import numpy as np
import ml_dtypes


def mxq(x, axis, fmt="e4m3"):
    dtype, down = {"e4m3": (ml_dtypes.float8_e4m3fn, 7), "e5m2": (ml_dtypes.float8_e5m2, 14)}[fmt]
    v = np.moveaxis(np.asarray(x, np.float32).astype(ml_dtypes.bfloat16).astype(np.float64), axis, -1)
    blocks = v.reshape(v.shape[:-1] + (-1, 32))
    amax = np.abs(blocks).max(-1, keepdims=True)
    byte = np.maximum(np.where(amax > 0, np.frexp(amax)[1] - 1 + 127, 0) - down, 1)
    scale = np.exp2(byte - 127.0)
    codes = (blocks / scale).astype(np.float32).astype(dtype).astype(np.float64)
    return np.moveaxis((codes * scale).reshape(v.shape), -1, axis)


WIDE = False


def mx_kscale(k):
    if not WIDE:
        return np.ones(k)
    levels = np.array([10, -10, 5, -5, 0])
    if k % 512:
        return np.exp2(np.random.permutation(np.resize(levels, k // 32))).repeat(32)
    a = np.empty((k // 512, 16))
    for p in range(k // 512):
        a[p, :8] = np.random.permutation(np.resize(levels, 8))
        for g in range(8):
            far = levels[np.abs(levels - a[p, g]) >= 10]
            a[p, g + 8] = far[np.random.randint(len(far))]
    return np.exp2(a.ravel()).repeat(32)


def f64(x):
    return np.asarray(x).astype(np.float64)


def striped(idx):
    return np.tile(idx.reshape(-1, 16).T, (8, 1)).astype(np.uint16)


def unstriped(offs):
    return offs[:16].T.reshape(-1).astype(np.int64)


E2M1 = np.array([0.0, 0.5, 1.0, 1.5, 2.0, 3.0, 4.0, 6.0, -0.0, -0.5, -1.0, -1.5, -2.0, -3.0, -4.0, -6.0])


def pack_weight(w, fmt):
    k, n = w.shape
    w = f64(np.asarray(w, np.float32).astype(ml_dtypes.bfloat16)).reshape(k // 32, 32, n)
    amax = np.abs(w).max(1)
    if fmt == "e4m3":
        byte = np.frexp(amax)[1] - 1 + 127 - 7
    else:
        mant, ex = np.frexp(amax / 6.0)
        byte = np.where(mant > 0.5, ex, ex - 1) + 127
    byte = np.clip(np.where(amax > 0, byte, 1), 1, 254)
    scaled = (w * np.exp2(127.0 - byte)[:, None, :]).reshape(k, n).astype(np.float32)
    by_word = np.ascontiguousarray(scaled.reshape(k // 512, 128, 4, n).transpose(0, 1, 3, 2))
    if fmt == "e4m3":
        words = by_word.astype(ml_dtypes.float8_e4m3fn).view(np.uint8)
    else:
        c = by_word.astype(ml_dtypes.float4_e2m1fn).view(np.uint8) & 0xF
        words = (c[..., 0::2] | (c[..., 1::2] << 4)).reshape(k // 512, 128, 2 * n)
    return np.ascontiguousarray(words), np.ascontiguousarray(byte.astype(np.uint8).reshape(k // 512, 16, n))


def unpack_weight(words, scales, fmt):
    g, _, n = scales.shape
    words = np.ascontiguousarray(words).reshape(g, 128, n, -1)
    if fmt == "e4m3":
        vals = words.view(ml_dtypes.float8_e4m3fn).astype(np.float64)
    else:
        nib = np.empty((g, 128, n, 4), np.uint8)
        nib[..., 0::2] = words & 0xF
        nib[..., 1::2] = words >> 4
        vals = E2M1[nib]
    vals = vals * np.repeat(np.exp2(scales.astype(np.float64) - 127.0), 8, axis=1)[..., None]
    return vals.transpose(0, 1, 3, 2).reshape(g * 512, n)


def relu(v):
    return np.maximum(v, 0.0)


def d_relu(v):
    return (v > 0).astype(np.float64)


K, T, E, C, H, N = 128, 1536, 6, 128, 512, 1024


def by_expert(wq, xq):
    return np.concatenate([wq[e].T @ xq[:, e * C:(e + 1) * C] for e in range(E)], axis=1)


def setup_inputs():
    n = np.random.standard_normal
    s = mx_kscale(N)[:, None]
    u = mx_kscale(H)
    dy = pack_weight(n((N, T)) * s, "e4m3")
    w2 = [pack_weight(m, "e2m1") for m in n((E, N, H)) / np.sqrt(N) / s[None] * u[None, None, :]]
    w1 = [pack_weight(m, "e2m1") for m in n((E, H, K)) / np.sqrt(H) / u[None, :, None]]
    w3 = [pack_weight(m, "e2m1") for m in n((E, H, K)) / np.sqrt(H) / u[None, :, None]]
    return {
        "dy_words": dy[0],
        "dy_scales": dy[1],
        "a1": n((H, E * C)).astype(np.float32),
        "a3": n((H, E * C)).astype(np.float32),
        "w2_words": np.stack([m[0] for m in w2]),
        "w2_scales": np.stack([m[1] for m in w2]),
        "w1_words": np.stack([m[0] for m in w1]),
        "w1_scales": np.stack([m[1] for m in w1]),
        "w3_words": np.stack([m[0] for m in w3]),
        "w3_scales": np.stack([m[1] for m in w3]),
        "gate": np.tile(np.random.uniform(0.2, 1.0, E * C), (H, 1)).astype(np.float32),
        "offs": striped(np.random.permutation(T)[:E * C]),
    }


def reference(dy_words, dy_scales, a1, a3, w2_words, w2_scales, w1_words, w1_scales, w3_words, w3_scales, gate, offs):
    idx = unstriped(offs)
    w2 = np.stack([unpack_weight(w2_words[e], w2_scales[e], "e2m1") for e in range(E)])
    w1 = np.stack([unpack_weight(w1_words[e], w1_scales[e], "e2m1") for e in range(E)])
    w3 = np.stack([unpack_weight(w3_words[e], w3_scales[e], "e2m1") for e in range(E)])
    gq = unpack_weight(dy_words, dy_scales, "e4m3")[:, idx]
    dh = f64(gate) * by_expert(w2, gq)
    da1 = dh * f64(a3) * d_relu(f64(a1))
    da3 = dh * relu(f64(a1))
    dx = by_expert(w1, mxq(da1, 0, "e4m3")) + by_expert(w3, mxq(da3, 0, "e4m3"))
    out = np.zeros((K, T))
    out[:, idx] = dx
    return out

@@ -1,0 +1,216 @@
+from contextlib import ExitStack
+
+import concourse.mybir as mybir
+from concourse.masks import make_identity
+
+K, T, E, C, H, N = 128, 1536, 6, 128, 512, 1024
+SLOTS = E * C
+FLOPS = 2 * SLOTS * (N * H + 2 * H * K)
+BYTES = 2 * 128 * T * 4 + 2 * 16 * T + 2 * H * SLOTS * 4 + E * (N * H + 2 * H * K) * 17 // 32 + SLOTS * 4 + 128 * SLOTS // 8 + K * T * 4
+
+F32 = mybir.dt.float32
+BF16 = mybir.dt.bfloat16
+I32 = mybir.dt.int32
+U32 = mybir.dt.uint32
+U16 = mybir.dt.uint16
+U8 = mybir.dt.uint8
+FP8X4 = mybir.dt.float8_e4m3fn_x4
+FP4X4 = mybir.dt.float4_e2m1fn_x4
+ALU = mybir.AluOpType
+ACT = mybir.ActivationFunctionType
+
+P = 128
+PACK = 4
+PASSES = N // (P * PACK)
+GROUPS = [(0, 1), (1, 3), (3, 5), (5, 6)]
+FIRST_SLOTS = 2 * C
+SCATTERS = [(0, 256), (256, 576), (576, 768)]
+
+
+def tile_moe_bdx_glu_relu_kernel(
+    tc, dy_words, dy_scales, a1, a3, w2_words, w2_scales, w1_words, w1_scales, w3_words, w3_scales, gate, offs, out
+):
+    nc = tc.nc
+    with ExitStack() as ctx:
+        keep = ctx.enter_context(tc.tile_pool(name="keep", bufs=1))
+        ring = ctx.enter_context(tc.tile_pool(name="ring", bufs=3))
+        ps_dh = ctx.enter_context(tc.psum_pool(name="ps_dh", bufs=2))
+        ps_turn = ctx.enter_context(tc.psum_pool(name="ps_turn", bufs=3))
+        ps_dx = ctx.enter_context(tc.psum_pool(name="ps_dx", bufs=2))
+        ps_gate = ctx.enter_context(tc.psum_pool(name="ps_gate", bufs=1))
+
+        group_of = {e: g for g, (lo, hi) in enumerate(GROUPS) for e in range(lo, hi)}
+        widths = [hi - lo for lo, hi in GROUPS]
+
+        offsets = keep.tile([P, SLOTS // 16], U16, name="offsets")
+        dy_w = [keep.tile([P, T], I32, name=f"dy_w{o}", align_bytes=64) for o in range(PASSES)]
+        dy_s = keep.tile([P, T], U8, name="dy_s", align_bytes=64)
+        w2_w = [keep.tile([P, w * PASSES, 2 * H], U8, name=f"w2_w{g}", align_bytes=64) for g, w in enumerate(widths)]
+        w2_s = keep.tile([P, E * PASSES, H], U8, name="w2_s", align_bytes=64)
+        w1_w = keep.tile([P, E, 2 * K], U8, name="w1_w", align_bytes=64)
+        w3_w = keep.tile([P, E, 2 * K], U8, name="w3_w", align_bytes=64)
+        w13_s = keep.tile([P, 2, E, K], U8, name="w13_s", align_bytes=64)
+        a1_t = [keep.tile([P, PACK, w * C], F32, name=f"a1_t{g}") for g, w in enumerate(widths)]
+        a3_t = [keep.tile([P, PACK, w * C], F32, name=f"a3_t{g}") for g, w in enumerate(widths)]
+        relu_a1 = [keep.tile([P, PACK, w * C], F32, name=f"relu_a1{g}") for g, w in enumerate(widths)]
+        masked_a3 = [keep.tile([P, PACK, w * C], F32, name=f"masked_a3{g}") for g, w in enumerate(widths)]
+        gate_rows = keep.tile([P, C], F32, name="gate_rows")
+        gate_cols = keep.tile([P, E], F32, name="gate_cols")
+        ident = keep.tile([P, P], F32, name="ident")
+        g_w = [keep.tile([P, SLOTS], U32, name=f"g_w{o}", align_bytes=64) for o in range(PASSES)]
+        g_s = [keep.tile([P, SLOTS], U8, name=f"g_s{o}", align_bytes=64) for o in range(PASSES)]
+        dx = keep.tile([P, SLOTS], F32, name="dx")
+        result = keep.tile([P, T], F32, name="result")
+
+        def zero(flat):
+            nc.vector.memset(flat.bitcast(I32), 0)
+
+        zero_col = keep.tile([P, 1], F32, name="zero_col")
+        nc.vector.memset(zero_col[:], 0.0)
+        zero(dy_s[:])
+        zero(w2_s[:].rearrange("p a i -> p (a i)"))
+        zero(w13_s[:].rearrange("p j e k -> p (j e k)"))
+        zero(g_s[1][:])
+        nc.scalar.activation(result[:], zero_col[:].to_broadcast([P, T]), ACT.Copy)
+        make_identity(nc, ident[:])
+
+        def load_scale_rows(queue, plane, scales_by_r, r):
+            queue.dma_start(out=plane[r:P:32].bitcast(I32), in_=scales_by_r[r].bitcast(I32))
+
+        w2_s_by_r = w2_scales.rearrange("e s (q r) i -> r q (e s) i", r=4)
+        w1_s_by_r = w1_scales.rearrange("e s (q r) k -> r q (e s) k", r=4)
+        w3_s_by_r = w3_scales.rearrange("e s (q r) k -> r q (e s) k", r=4)
+        a1_v = a1.rearrange("(p t) s -> p t s", t=PACK)
+        a3_v = a3.rearrange("(p t) s -> p t s", t=PACK)
+        w2_v = w2_words.rearrange("e s p b -> p (e s) b")
+
+        for r in range(4):
+            load_scale_rows(nc.gpsimd, w2_s, w2_s_by_r, r)
+
+        nc.sync.dma_start(offsets[:], offs)
+        for q in range(4):
+            nc.sync.dma_start(
+                out=dy_s[32 * q : 32 * q + 4 * PASSES, :].bitcast(I32),
+                in_=dy_scales[:, 4 * q : 4 * q + 4, :].bitcast(I32),
+            )
+        nc.sync.dma_start(out=gate_rows[:], in_=gate.rearrange("h (e c) -> (h e) c", c=C)[0:P, :])
+        for o in range(PASSES):
+            nc.sync.dma_start(out=dy_w[o][:], in_=dy_words[o].rearrange("p t d -> p (t d)").bitcast(I32))
+        small = [(j, r) for r in range(4) for j in range(2)]
+
+        def load_small(count):
+            for j, r in small[:count]:
+                load_scale_rows(nc.sync, w13_s[:, j], (w1_s_by_r, w3_s_by_r)[j], r)
+            for pair in small[:count]:
+                small.remove(pair)
+
+        for g, (lo, hi) in enumerate(GROUPS):
+            nc.sync.dma_start(out=w2_w[g][:].bitcast(I32), in_=w2_v[:, lo * PASSES : hi * PASSES, :].bitcast(I32))
+            if g == 1:
+                load_small(2)
+            nc.sync.dma_start(out=a1_t[g][:], in_=a1_v[:, :, lo * C : hi * C])
+            if g == 1:
+                load_small(2)
+            nc.sync.dma_start(out=a3_t[g][:], in_=a3_v[:, :, lo * C : hi * C])
+            if g == 1:
+                load_small(2)
+                nc.sync.dma_start(out=w1_w[:].bitcast(I32), in_=w1_words.rearrange("e s p b -> p (e s) b").bitcast(I32))
+                load_small(2)
+                nc.sync.dma_start(out=w3_w[:].bitcast(I32), in_=w3_words.rearrange("e s p b -> p (e s) b").bitcast(I32))
+
+        gate_ps = ps_gate.tile([P, P], F32, name="gate_ps")
+        nc.tensor.transpose(gate_ps[:], gate_rows[:], ident[:])
+        nc.scalar.activation(gate_cols[:], gate_ps[:, 0:E], ACT.Copy)
+
+        def gather_words(o, lo, hi):
+            nc.vector.tensor_copy(g_w[o][:, lo:hi], dy_w[o][:].bitcast(U32).indirect(offsets[:, lo // 16 : hi // 16]))
+
+        nc.vector.tensor_copy(g_s[0][:], dy_s[:].indirect(offsets[:]))
+        for r in range(4):
+            nc.scalar.dma_start(out=g_s[1][r:P:32, :].bitcast(I32), in_=g_s[0][4 + r : P : 32, :].bitcast(I32))
+        for lo, hi in ((0, FIRST_SLOTS), (FIRST_SLOTS, SLOTS)):
+            for o in range(PASSES):
+                gather_words(o, lo, hi)
+
+        turned = {}
+        da = {}
+
+        def local(e):
+            return e - GROUPS[group_of[e]][0]
+
+        def first_product(e):
+            slots = slice(e * C, (e + 1) * C)
+            dh_ps = ps_dh.tile([P, H], F32, name="dh_ps")
+            for o in range(PASSES):
+                nc.tensor.matmul_mx(
+                    out=dh_ps[:],
+                    lhsT=g_w[o][:, slots].bitcast(FP8X4),
+                    lhsT_scale=g_s[o][:, slots],
+                    rhs=w2_w[group_of[e]][:, local(e) * PASSES + o, :].bitcast(FP4X4),
+                    rhs_scale=w2_s[:, e * PASSES + o, :],
+                    start=(o == 0),
+                    stop=(o == PASSES - 1),
+                )
+            dh_rows = ring.tile([P, PACK, P], F32, name="dh_rows")
+            nc.scalar.activation(
+                dh_rows[:], dh_ps[:].rearrange("s (m t) -> s t m", t=PACK), ACT.Copy, scale=gate_cols[:, e : e + 1]
+            )
+            turned[e] = ps_turn.tile([P, PACK, C], F32, name="turned")
+            for t in range(PACK):
+                nc.tensor.transpose(turned[e][:, t, :], dh_rows[:, t, :], ident[:])
+
+        def factors(g):
+            nc.scalar.activation(relu_a1[g][:], a1_t[g][:], ACT.Relu)
+            nc.vector.scalar_tensor_tensor(masked_a3[g][:], a1_t[g][:], 0.0, a3_t[g][:], ALU.is_gt, ALU.mult)
+
+        def gradients(e):
+            da[e] = ring.tile([P, 2, C, PACK], BF16, name="da", align_bytes=64)
+            cols = slice(local(e) * C, (local(e) + 1) * C)
+            for j, factor in enumerate((masked_a3, relu_a1)):
+                nc.vector.tensor_tensor(
+                    da[e][:, j].rearrange("p (c i) t -> p c t i", i=2),
+                    turned[e][:].rearrange("p t (c i) -> p c t i", i=2),
+                    factor[group_of[e]][:, :, cols].rearrange("p t (c i) -> p c t i", i=2),
+                    ALU.mult,
+                )
+
+        def second_product(e):
+            codes = ring.tile([P, 2, C], U32, name="codes", align_bytes=64)
+            scales = ring.tile([P, 2, C], U8, name="scales", align_bytes=64)
+            nc.vector.quantize_mx(
+                out=codes[:].rearrange("p j s -> p (j s)").bitcast(FP8X4),
+                scales=scales[:].rearrange("p j s -> p (j s)"),
+                in_=da[e][:].rearrange("p j s t -> p (j s t)"),
+            )
+            dx_ps = ps_dx.tile([P, C], F32, name="dx_ps")
+            for j, weights in enumerate((w1_w, w3_w)):
+                nc.tensor.matmul_mx(
+                    out=dx_ps[:],
+                    lhsT=weights[:, e, :].bitcast(FP4X4),
+                    lhsT_scale=w13_s[:, j, e, :],
+                    rhs=codes[:, j, :].bitcast(FP8X4),
+                    rhs_scale=scales[:, j, :],
+                    start=(j == 0),
+                    stop=(j == 1),
+                )
+            nc.scalar.copy(dx[:, e * C : (e + 1) * C], dx_ps[:])
+
+        def scatter(lo, hi):
+            nc.vector.tensor_copy(result[:].indirect(offsets[:, lo // 16 : hi // 16]), dx[:, lo:hi])
+
+        first_product(0)
+        first_product(1)
+        for e in range(E):
+            if local(e) == 0:
+                factors(group_of[e])
+            if e + 2 < E:
+                first_product(e + 2)
+            gradients(e)
+            if e >= 1:
+                second_product(e - 1)
+            if e == 3:
+                scatter(*SCATTERS[0])
+        second_product(E - 1)
+        scatter(*SCATTERS[1])
+        scatter(*SCATTERS[2])
+        nc.sync.dma_start(out=out, in_=result[:])

@@ -44,7 +44,7 @@ def tile_moe_bdx_glu_relu_kernel(
 
         offsets = keep.tile([P, SLOTS // 16], U16, name="offsets")
         dy_w = [keep.tile([P, T], I32, name=f"dy_w{o}", align_bytes=64) for o in range(PASSES)]
-        dy_s = keep.tile([P, T], U8, name="dy_s", align_bytes=64)
+        dy_s = keep.tile([P, PASSES, T], U8, name="dy_s", align_bytes=64)
         w2_w = [keep.tile([P, w * PASSES, 2 * H], U8, name=f"w2_w{g}", align_bytes=64) for g, w in enumerate(widths)]
         w2_s = keep.tile([P, E * PASSES, H], U8, name="w2_s", align_bytes=64)
         w1_w = keep.tile([P, E, 2 * K], U8, name="w1_w", align_bytes=64)
@@ -52,8 +52,9 @@ def tile_moe_bdx_glu_relu_kernel(
         w13_s = keep.tile([P, 2, E, K], U8, name="w13_s", align_bytes=64)
         a1_t = [keep.tile([P, PACK, w * C], F32, name=f"a1_t{g}") for g, w in enumerate(widths)]
         a3_t = [keep.tile([P, PACK, w * C], F32, name=f"a3_t{g}") for g, w in enumerate(widths)]
-        relu_a1 = [keep.tile([P, PACK, w * C], F32, name=f"relu_a1{g}") for g, w in enumerate(widths)]
-        masked_a3 = [keep.tile([P, PACK, w * C], F32, name=f"masked_a3{g}") for g, w in enumerate(widths)]
+        factor = [keep.tile([P, 2, C, PACK], F32, name=f"factor{e}") for e in range(E)]
+        codes = [keep.tile([P, 2, C], U32, name=f"codes{e}", align_bytes=64) for e in range(E)]
+        scales = [keep.tile([P, 2, C], U8, name=f"scales{e}", align_bytes=64) for e in range(E)]
         gate_rows = keep.tile([P, C], F32, name="gate_rows")
         gate_cols = keep.tile([P, E], F32, name="gate_cols")
         ident = keep.tile([P, P], F32, name="ident")
@@ -67,10 +68,9 @@ def tile_moe_bdx_glu_relu_kernel(
 
         zero_col = keep.tile([P, 1], F32, name="zero_col")
         nc.vector.memset(zero_col[:], 0.0)
-        zero(dy_s[:])
+        zero(dy_s[:].rearrange("p o t -> p (o t)"))
         zero(w2_s[:].rearrange("p a i -> p (a i)"))
         zero(w13_s[:].rearrange("p j e k -> p (j e k)"))
-        zero(g_s[1][:])
         nc.scalar.activation(result[:], zero_col[:].to_broadcast([P, T]), ACT.Copy)
         make_identity(nc, ident[:])
 
@@ -84,39 +84,28 @@ def tile_moe_bdx_glu_relu_kernel(
         a3_v = a3.rearrange("(p t) s -> p t s", t=PACK)
         w2_v = w2_words.rearrange("e s p b -> p (e s) b")
 
-        for r in range(4):
-            load_scale_rows(nc.gpsimd, w2_s, w2_s_by_r, r)
+        dy_s_by_r = dy_scales.rearrange("o (q r) t -> r q o t", r=4)
+
+        def load_dy_words(o):
+            nc.sync.dma_start(out=dy_w[o][:], in_=dy_words[o].rearrange("p t d -> p (t d)").bitcast(I32))
 
         nc.sync.dma_start(offsets[:], offs)
-        for q in range(4):
-            nc.sync.dma_start(
-                out=dy_s[32 * q : 32 * q + 4 * PASSES, :].bitcast(I32),
-                in_=dy_scales[:, 4 * q : 4 * q + 4, :].bitcast(I32),
-            )
+        load_dy_words(0)
+        for r in range(4):
+            load_scale_rows(nc.sync, dy_s, dy_s_by_r, r)
+        load_dy_words(1)
         nc.sync.dma_start(out=gate_rows[:], in_=gate.rearrange("h (e c) -> (h e) c", c=C)[0:P, :])
-        for o in range(PASSES):
-            nc.sync.dma_start(out=dy_w[o][:], in_=dy_words[o].rearrange("p t d -> p (t d)").bitcast(I32))
-        small = [(j, r) for r in range(4) for j in range(2)]
-
-        def load_small(count):
-            for j, r in small[:count]:
-                load_scale_rows(nc.sync, w13_s[:, j], (w1_s_by_r, w3_s_by_r)[j], r)
-            for pair in small[:count]:
-                small.remove(pair)
-
+        for r in range(4):
+            load_scale_rows(nc.sync, w2_s, w2_s_by_r, r)
         for g, (lo, hi) in enumerate(GROUPS):
             nc.sync.dma_start(out=w2_w[g][:].bitcast(I32), in_=w2_v[:, lo * PASSES : hi * PASSES, :].bitcast(I32))
-            if g == 1:
-                load_small(2)
             nc.sync.dma_start(out=a1_t[g][:], in_=a1_v[:, :, lo * C : hi * C])
-            if g == 1:
-                load_small(2)
             nc.sync.dma_start(out=a3_t[g][:], in_=a3_v[:, :, lo * C : hi * C])
-            if g == 1:
-                load_small(2)
-                nc.sync.dma_start(out=w1_w[:].bitcast(I32), in_=w1_words.rearrange("e s p b -> p (e s) b").bitcast(I32))
-                load_small(2)
-                nc.sync.dma_start(out=w3_w[:].bitcast(I32), in_=w3_words.rearrange("e s p b -> p (e s) b").bitcast(I32))
+        nc.sync.dma_start(out=w1_w[:].bitcast(I32), in_=w1_words.rearrange("e s p b -> p (e s) b").bitcast(I32))
+        nc.sync.dma_start(out=w3_w[:].bitcast(I32), in_=w3_words.rearrange("e s p b -> p (e s) b").bitcast(I32))
+        for r in range(4):
+            load_scale_rows(nc.sync, w13_s[:, 0], w1_s_by_r, r)
+            load_scale_rows(nc.sync, w13_s[:, 1], w3_s_by_r, r)
 
         gate_ps = ps_gate.tile([P, P], F32, name="gate_ps")
         nc.tensor.transpose(gate_ps[:], gate_rows[:], ident[:])
@@ -125,12 +114,14 @@ def tile_moe_bdx_glu_relu_kernel(
         def gather_words(o, lo, hi):
             nc.vector.tensor_copy(g_w[o][:, lo:hi], dy_w[o][:].bitcast(U32).indirect(offsets[:, lo // 16 : hi // 16]))
 
-        nc.vector.tensor_copy(g_s[0][:], dy_s[:].indirect(offsets[:]))
-        for r in range(4):
-            nc.scalar.dma_start(out=g_s[1][r:P:32, :].bitcast(I32), in_=g_s[0][4 + r : P : 32, :].bitcast(I32))
+        def gather_scales(o, lo, hi):
+            nc.vector.tensor_copy(g_s[o][:, lo:hi], dy_s[:, o, :].indirect(offsets[:, lo // 16 : hi // 16]))
+
+        gather_words(0, 0, SLOTS)
+        gather_scales(0, 0, SLOTS)
         for lo, hi in ((0, FIRST_SLOTS), (FIRST_SLOTS, SLOTS)):
-            for o in range(PASSES):
-                gather_words(o, lo, hi)
+            gather_scales(1, lo, hi)
+            gather_words(1, lo, hi)
 
         turned = {}
         da = {}
@@ -159,37 +150,43 @@ def tile_moe_bdx_glu_relu_kernel(
             for t in range(PACK):
                 nc.tensor.transpose(turned[e][:, t, :], dh_rows[:, t, :], ident[:])
 
-        def factors(g):
-            nc.scalar.activation(relu_a1[g][:], a1_t[g][:], ACT.Relu)
-            nc.vector.scalar_tensor_tensor(masked_a3[g][:], a1_t[g][:], 0.0, a3_t[g][:], ALU.is_gt, ALU.mult)
+        def factors(e):
+            cols = slice(local(e) * C, (local(e) + 1) * C)
+            nc.scalar.activation(factor[e][:, 1], a1_t[group_of[e]][:, :, cols].rearrange("p t s -> p s t"), ACT.Relu)
+            nc.vector.scalar_tensor_tensor(
+                factor[e][:, 0],
+                factor[e][:, 1],
+                0.0,
+                a3_t[group_of[e]][:, :, cols].rearrange("p t s -> p s t"),
+                ALU.is_gt,
+                ALU.mult,
+            )
 
         def gradients(e):
             da[e] = ring.tile([P, 2, C, PACK], BF16, name="da", align_bytes=64)
-            cols = slice(local(e) * C, (local(e) + 1) * C)
-            for j, factor in enumerate((masked_a3, relu_a1)):
-                nc.vector.tensor_tensor(
-                    da[e][:, j].rearrange("p (c i) t -> p c t i", i=2),
-                    turned[e][:].rearrange("p t (c i) -> p c t i", i=2),
-                    factor[group_of[e]][:, :, cols].rearrange("p t (c i) -> p c t i", i=2),
-                    ALU.mult,
-                )
+            nc.vector.tensor_tensor(
+                da[e][:],
+                turned[e][:].rearrange("p t s -> p s t").unsqueeze(1).to_broadcast([P, 2, C, PACK]),
+                factor[e][:],
+                ALU.mult,
+            )
 
-        def second_product(e):
-            codes = ring.tile([P, 2, C], U32, name="codes", align_bytes=64)
-            scales = ring.tile([P, 2, C], U8, name="scales", align_bytes=64)
+        def quantise(e):
             nc.vector.quantize_mx(
-                out=codes[:].rearrange("p j s -> p (j s)").bitcast(FP8X4),
-                scales=scales[:].rearrange("p j s -> p (j s)"),
+                out=codes[e][:].rearrange("p j s -> p (j s)").bitcast(FP8X4),
+                scales=scales[e][:].rearrange("p j s -> p (j s)"),
                 in_=da[e][:].rearrange("p j s t -> p (j s t)"),
             )
+
+        def second_product(e):
             dx_ps = ps_dx.tile([P, C], F32, name="dx_ps")
             for j, weights in enumerate((w1_w, w3_w)):
                 nc.tensor.matmul_mx(
                     out=dx_ps[:],
                     lhsT=weights[:, e, :].bitcast(FP4X4),
                     lhsT_scale=w13_s[:, j, e, :],
-                    rhs=codes[:, j, :].bitcast(FP8X4),
-                    rhs_scale=scales[:, j, :],
+                    rhs=codes[e][:, j, :].bitcast(FP8X4),
+                    rhs_scale=scales[e][:, j, :],
                     start=(j == 0),
                     stop=(j == 1),
                 )
@@ -199,18 +196,19 @@ def tile_moe_bdx_glu_relu_kernel(
             nc.vector.tensor_copy(result[:].indirect(offsets[:, lo // 16 : hi // 16]), dx[:, lo:hi])
 
         first_product(0)
+        factors(0)
         first_product(1)
         for e in range(E):
-            if local(e) == 0:
-                factors(group_of[e])
+            if e + 1 < E:
+                factors(e + 1)
             if e + 2 < E:
                 first_product(e + 2)
             gradients(e)
             if e >= 1:
-                second_product(e - 1)
-            if e == 3:
-                scatter(*SCATTERS[0])
-        second_product(E - 1)
-        scatter(*SCATTERS[1])
-        scatter(*SCATTERS[2])
+                quantise(e - 1)
+        quantise(E - 1)
+        for e in range(E):
+            second_product(e)
+        for lo, hi in SCATTERS:
+            scatter(lo, hi)
         nc.sync.dma_start(out=out, in_=result[:])

@@ -22,9 +22,10 @@ ACT = mybir.ActivationFunctionType
 P = 128
 PACK = 4
 PASSES = N // (P * PACK)
-GROUPS = [(0, 1), (1, 3), (3, 5), (5, 6)]
+GROUPS = [(0, 2), (2, 4), (4, 6)]
+EARLY = 2 * PASSES
 FIRST_SLOTS = 2 * C
-SCATTERS = [(0, 256), (256, 576), (576, 768)]
+SCATTERS = [(0, 256), (256, 512), (512, 768)]
 
 
 def tile_moe_bdx_glu_relu_kernel(
@@ -34,6 +35,7 @@ def tile_moe_bdx_glu_relu_kernel(
     with ExitStack() as ctx:
         keep = ctx.enter_context(tc.tile_pool(name="keep", bufs=1))
         ring = ctx.enter_context(tc.tile_pool(name="ring", bufs=3))
+        two = ctx.enter_context(tc.tile_pool(name="two", bufs=2))
         ps_dh = ctx.enter_context(tc.psum_pool(name="ps_dh", bufs=2))
         ps_turn = ctx.enter_context(tc.psum_pool(name="ps_turn", bufs=3))
         ps_dx = ctx.enter_context(tc.psum_pool(name="ps_dx", bufs=2))
@@ -46,13 +48,13 @@ def tile_moe_bdx_glu_relu_kernel(
         dy_w = [keep.tile([P, T], I32, name=f"dy_w{o}", align_bytes=64) for o in range(PASSES)]
         dy_s = keep.tile([P, PASSES, T], U8, name="dy_s", align_bytes=64)
         w2_w = [keep.tile([P, w * PASSES, 2 * H], U8, name=f"w2_w{g}", align_bytes=64) for g, w in enumerate(widths)]
-        w2_s = keep.tile([P, E * PASSES, H], U8, name="w2_s", align_bytes=64)
+        w2_s_early = keep.tile([P, EARLY, H], U8, name="w2_s_early", align_bytes=64)
+        w2_s_late = keep.tile([P, E * PASSES - EARLY, H], U8, name="w2_s_late", align_bytes=64)
         w1_w = keep.tile([P, E, 2 * K], U8, name="w1_w", align_bytes=64)
         w3_w = keep.tile([P, E, 2 * K], U8, name="w3_w", align_bytes=64)
         w13_s = keep.tile([P, 2, E, K], U8, name="w13_s", align_bytes=64)
         a1_t = [keep.tile([P, PACK, w * C], F32, name=f"a1_t{g}") for g, w in enumerate(widths)]
         a3_t = [keep.tile([P, PACK, w * C], F32, name=f"a3_t{g}") for g, w in enumerate(widths)]
-        factor = [keep.tile([P, 2, C, PACK], F32, name=f"factor{e}") for e in range(E)]
         codes = [keep.tile([P, 2, C], U32, name=f"codes{e}", align_bytes=64) for e in range(E)]
         scales = [keep.tile([P, 2, C], U8, name=f"scales{e}", align_bytes=64) for e in range(E)]
         gate_rows = keep.tile([P, C], F32, name="gate_rows")
@@ -67,9 +69,10 @@ def tile_moe_bdx_glu_relu_kernel(
             nc.vector.memset(flat.bitcast(I32), 0)
 
         zero_col = keep.tile([P, 1], F32, name="zero_col")
-        nc.vector.memset(zero_col[:], 0.0)
         zero(dy_s[:].rearrange("p o t -> p (o t)"))
-        zero(w2_s[:].rearrange("p a i -> p (a i)"))
+        nc.vector.memset(zero_col[:], 0.0)
+        zero(w2_s_early[:].rearrange("p a i -> p (a i)"))
+        zero(w2_s_late[:].rearrange("p a i -> p (a i)"))
         zero(w13_s[:].rearrange("p j e k -> p (j e k)"))
         nc.scalar.activation(result[:], zero_col[:].to_broadcast([P, T]), ACT.Copy)
         make_identity(nc, ident[:])
@@ -96,16 +99,26 @@ def tile_moe_bdx_glu_relu_kernel(
         load_dy_words(1)
         nc.sync.dma_start(out=gate_rows[:], in_=gate.rearrange("h (e c) -> (h e) c", c=C)[0:P, :])
         for r in range(4):
-            load_scale_rows(nc.sync, w2_s, w2_s_by_r, r)
-        for g, (lo, hi) in enumerate(GROUPS):
-            nc.sync.dma_start(out=w2_w[g][:].bitcast(I32), in_=w2_v[:, lo * PASSES : hi * PASSES, :].bitcast(I32))
-            nc.sync.dma_start(out=a1_t[g][:], in_=a1_v[:, :, lo * C : hi * C])
-            nc.sync.dma_start(out=a3_t[g][:], in_=a3_v[:, :, lo * C : hi * C])
-        nc.sync.dma_start(out=w1_w[:].bitcast(I32), in_=w1_words.rearrange("e s p b -> p (e s) b").bitcast(I32))
-        nc.sync.dma_start(out=w3_w[:].bitcast(I32), in_=w3_words.rearrange("e s p b -> p (e s) b").bitcast(I32))
+            load_scale_rows(nc.sync, w2_s_early, w2_s_by_r[:, :, :EARLY], r)
         for r in range(4):
-            load_scale_rows(nc.sync, w13_s[:, 0], w1_s_by_r, r)
-            load_scale_rows(nc.sync, w13_s[:, 1], w3_s_by_r, r)
+            load_scale_rows(nc.gpsimd, w2_s_late, w2_s_by_r[:, :, EARLY:], r)
+        def load_w2(g):
+            lo, hi = GROUPS[g]
+            nc.sync.dma_start(out=w2_w[g][:].bitcast(I32), in_=w2_v[:, lo * PASSES : hi * PASSES, :].bitcast(I32))
+
+        def load_saved(tiles, view, g):
+            lo, hi = GROUPS[g]
+            nc.sync.dma_start(out=tiles[g][:], in_=view[:, :, lo * C : hi * C])
+
+        for g in range(len(GROUPS)):
+            load_w2(g)
+            load_saved(a1_t, a1_v, g)
+            load_saved(a3_t, a3_v, g)
+        for tile, words in ((w1_w, w1_words), (w3_w, w3_words)):
+            nc.sync.dma_start(out=tile[:].bitcast(I32), in_=words.rearrange("e s p b -> p (e s) b").bitcast(I32))
+        for r in range(4):
+            load_scale_rows(nc.gpsimd, w13_s[:, 0], w1_s_by_r, r)
+            load_scale_rows(nc.gpsimd, w13_s[:, 1], w3_s_by_r, r)
 
         gate_ps = ps_gate.tile([P, P], F32, name="gate_ps")
         nc.tensor.transpose(gate_ps[:], gate_rows[:], ident[:])
@@ -124,10 +137,14 @@ def tile_moe_bdx_glu_relu_kernel(
             gather_words(1, lo, hi)
 
         turned = {}
+        factor = {}
         da = {}
 
         def local(e):
             return e - GROUPS[group_of[e]][0]
+
+        def w2_scale_plane(a):
+            return w2_s_early[:, a, :] if a < EARLY else w2_s_late[:, a - EARLY, :]
 
         def first_product(e):
             slots = slice(e * C, (e + 1) * C)
@@ -138,7 +155,7 @@ def tile_moe_bdx_glu_relu_kernel(
                     lhsT=g_w[o][:, slots].bitcast(FP8X4),
                     lhsT_scale=g_s[o][:, slots],
                     rhs=w2_w[group_of[e]][:, local(e) * PASSES + o, :].bitcast(FP4X4),
-                    rhs_scale=w2_s[:, e * PASSES + o, :],
+                    rhs_scale=w2_scale_plane(e * PASSES + o),
                     start=(o == 0),
                     stop=(o == PASSES - 1),
                 )
@@ -151,16 +168,11 @@ def tile_moe_bdx_glu_relu_kernel(
                 nc.tensor.transpose(turned[e][:, t, :], dh_rows[:, t, :], ident[:])
 
         def factors(e):
+            factor[e] = two.tile([P, 2, C, PACK], F32, name="factor")
             cols = slice(local(e) * C, (local(e) + 1) * C)
             nc.scalar.activation(factor[e][:, 1], a1_t[group_of[e]][:, :, cols].rearrange("p t s -> p s t"), ACT.Relu)
-            nc.vector.scalar_tensor_tensor(
-                factor[e][:, 0],
-                factor[e][:, 1],
-                0.0,
-                a3_t[group_of[e]][:, :, cols].rearrange("p t s -> p s t"),
-                ALU.is_gt,
-                ALU.mult,
-            )
+            a3_e = a3_t[group_of[e]][:, :, cols].rearrange("p t s -> p s t")
+            nc.vector.scalar_tensor_tensor(factor[e][:, 0], factor[e][:, 1], 0.0, a3_e, ALU.is_gt, ALU.mult)
 
         def gradients(e):
             da[e] = ring.tile([P, 2, C, PACK], BF16, name="da", align_bytes=64)
@@ -199,14 +211,12 @@ def tile_moe_bdx_glu_relu_kernel(
         factors(0)
         first_product(1)
         for e in range(E):
-            if e + 1 < E:
-                factors(e + 1)
             if e + 2 < E:
                 first_product(e + 2)
             gradients(e)
-            if e >= 1:
-                quantise(e - 1)
-        quantise(E - 1)
+            if e + 1 < E:
+                factors(e + 1)
+            quantise(e)
         for e in range(E):
             second_product(e)
         for lo, hi in SCATTERS:

@@ -75,6 +75,8 @@ def tile_moe_bdx_glu_relu_kernel(
         zero(w2_s_late[:].rearrange("p a i -> p (a i)"))
         zero(w13_s[:].rearrange("p j e k -> p (j e k)"))
         nc.scalar.activation(result[:], zero_col[:].to_broadcast([P, T]), ACT.Copy)
+        nc.gpsimd.memset(gate_rows[:], 0.0)
+        nc.gpsimd.dma_start(out=gate_rows[0:E, :], in_=gate[0].rearrange("(e c) -> e c", c=C))
         make_identity(nc, ident[:])
 
         def load_scale_rows(queue, plane, scales_by_r, r):
@@ -93,15 +95,13 @@ def tile_moe_bdx_glu_relu_kernel(
             nc.sync.dma_start(out=dy_w[o][:], in_=dy_words[o].rearrange("p t d -> p (t d)").bitcast(I32))
 
         nc.sync.dma_start(offsets[:], offs)
-        load_dy_words(0)
         for r in range(4):
             load_scale_rows(nc.sync, dy_s, dy_s_by_r, r)
+        load_dy_words(0)
         load_dy_words(1)
-        nc.sync.dma_start(out=gate_rows[:], in_=gate.rearrange("h (e c) -> (h e) c", c=C)[0:P, :])
-        for r in range(4):
-            load_scale_rows(nc.sync, w2_s_early, w2_s_by_r[:, :, :EARLY], r)
         for r in range(4):
             load_scale_rows(nc.gpsimd, w2_s_late, w2_s_by_r[:, :, EARLY:], r)
+
         def load_w2(g):
             lo, hi = GROUPS[g]
             nc.sync.dma_start(out=w2_w[g][:].bitcast(I32), in_=w2_v[:, lo * PASSES : hi * PASSES, :].bitcast(I32))
@@ -111,11 +111,15 @@ def tile_moe_bdx_glu_relu_kernel(
             nc.sync.dma_start(out=tiles[g][:], in_=view[:, :, lo * C : hi * C])
 
         for g in range(len(GROUPS)):
+            if g == len(GROUPS) - 1:
+                for tile, words in ((w1_w, w1_words), (w3_w, w3_words)):
+                    nc.sync.dma_start(out=tile[:].bitcast(I32), in_=words.rearrange("e s p b -> p (e s) b").bitcast(I32))
             load_w2(g)
+            if g == 0:
+                for r in range(4):
+                    load_scale_rows(nc.sync, w2_s_early, w2_s_by_r[:, :, :EARLY], r)
             load_saved(a1_t, a1_v, g)
             load_saved(a3_t, a3_v, g)
-        for tile, words in ((w1_w, w1_words), (w3_w, w3_words)):
-            nc.sync.dma_start(out=tile[:].bitcast(I32), in_=words.rearrange("e s p b -> p (e s) b").bitcast(I32))
         for r in range(4):
             load_scale_rows(nc.gpsimd, w13_s[:, 0], w1_s_by_r, r)
             load_scale_rows(nc.gpsimd, w13_s[:, 1], w3_s_by_r, r)
@@ -130,14 +134,15 @@ def tile_moe_bdx_glu_relu_kernel(
         def gather_scales(o, lo, hi):
             nc.vector.tensor_copy(g_s[o][:, lo:hi], dy_s[:, o, :].indirect(offsets[:, lo // 16 : hi // 16]))
 
-        gather_words(0, 0, SLOTS)
-        gather_scales(0, 0, SLOTS)
+        for o in range(PASSES):
+            gather_scales(o, 0, SLOTS)
         for lo, hi in ((0, FIRST_SLOTS), (FIRST_SLOTS, SLOTS)):
-            gather_scales(1, lo, hi)
-            gather_words(1, lo, hi)
+            for o in range(PASSES):
+                gather_words(o, lo, hi)
 
         turned = {}
-        factor = {}
+        masked = {}
+        relu = {}
         da = {}
 
         def local(e):
@@ -167,21 +172,24 @@ def tile_moe_bdx_glu_relu_kernel(
             for t in range(PACK):
                 nc.tensor.transpose(turned[e][:, t, :], dh_rows[:, t, :], ident[:])
 
-        def factors(e):
-            factor[e] = two.tile([P, 2, C, PACK], F32, name="factor")
-            cols = slice(local(e) * C, (local(e) + 1) * C)
-            nc.scalar.activation(factor[e][:, 1], a1_t[group_of[e]][:, :, cols].rearrange("p t s -> p s t"), ACT.Relu)
-            a3_e = a3_t[group_of[e]][:, :, cols].rearrange("p t s -> p s t")
-            nc.vector.scalar_tensor_tensor(factor[e][:, 0], factor[e][:, 1], 0.0, a3_e, ALU.is_gt, ALU.mult)
+        def masked_a3(g):
+            masked[g] = two.tile([P, PACK, widths[g] * C], F32, name="masked")
+            nc.vector.scalar_tensor_tensor(masked[g][:], a1_t[g][:], 0.0, a3_t[g][:], ALU.is_gt, ALU.mult)
+
+        def relu_a1(e):
+            relu[e] = ring.tile([P, PACK, C], F32, name="relu")
+            nc.scalar.activation(relu[e][:], a1_t[group_of[e]][:, :, local(e) * C : (local(e) + 1) * C], ACT.Relu)
+
+        def by_pairs(planes):
+            return planes.rearrange("p t (c i) -> p c t i", i=2)
 
         def gradients(e):
             da[e] = ring.tile([P, 2, C, PACK], BF16, name="da", align_bytes=64)
-            nc.vector.tensor_tensor(
-                da[e][:],
-                turned[e][:].rearrange("p t s -> p s t").unsqueeze(1).to_broadcast([P, 2, C, PACK]),
-                factor[e][:],
-                ALU.mult,
-            )
+            cols = slice(local(e) * C, (local(e) + 1) * C)
+            for j, factor in enumerate((masked[group_of[e]][:, :, cols], relu[e][:])):
+                nc.vector.tensor_tensor(
+                    da[e][:, j].rearrange("p (c i) t -> p c t i", i=2), by_pairs(turned[e][:]), by_pairs(factor), ALU.mult
+                )
 
         def quantise(e):
             nc.vector.quantize_mx(
@@ -208,17 +216,23 @@ def tile_moe_bdx_glu_relu_kernel(
             nc.vector.tensor_copy(result[:].indirect(offsets[:, lo // 16 : hi // 16]), dx[:, lo:hi])
 
         first_product(0)
-        factors(0)
+        relu_a1(0)
         first_product(1)
         for e in range(E):
+            if local(e) == 0:
+                masked_a3(group_of[e])
+            if e + 1 < E:
+                relu_a1(e + 1)
             if e + 2 < E:
                 first_product(e + 2)
             gradients(e)
-            if e + 1 < E:
-                factors(e + 1)
-            quantise(e)
-        for e in range(E):
-            second_product(e)
-        for lo, hi in SCATTERS:
+            if e > 0:
+                quantise(e - 1)
+                second_product(e - 1)
+            if e == 3:
+                scatter(*SCATTERS[0])
+        quantise(E - 1)
+        second_product(E - 1)
+        for lo, hi in SCATTERS[1:]:
             scatter(lo, hi)
         nc.sync.dma_start(out=out, in_=result[:])

@@ -37,7 +37,7 @@ def tile_moe_bdx_glu_relu_kernel(
         ring = ctx.enter_context(tc.tile_pool(name="ring", bufs=3))
         two = ctx.enter_context(tc.tile_pool(name="two", bufs=2))
         ps_dh = ctx.enter_context(tc.psum_pool(name="ps_dh", bufs=2))
-        ps_turn = ctx.enter_context(tc.psum_pool(name="ps_turn", bufs=3))
+        ps_turn = ctx.enter_context(tc.psum_pool(name="ps_turn", bufs=1))
         ps_dx = ctx.enter_context(tc.psum_pool(name="ps_dx", bufs=2))
         ps_gate = ctx.enter_context(tc.psum_pool(name="ps_gate", bufs=1))
 
@@ -69,7 +69,8 @@ def tile_moe_bdx_glu_relu_kernel(
             nc.vector.memset(flat.bitcast(I32), 0)
 
         zero_col = keep.tile([P, 1], F32, name="zero_col")
-        zero(dy_s[:].rearrange("p o t -> p (o t)"))
+        zero(dy_s[:, 0, :])
+        nc.gpsimd.memset(dy_s[:, 1, :].bitcast(I32), 0)
         nc.vector.memset(zero_col[:], 0.0)
         zero(w2_s_early[:].rearrange("p a i -> p (a i)"))
         zero(w2_s_late[:].rearrange("p a i -> p (a i)"))
@@ -168,7 +169,7 @@ def tile_moe_bdx_glu_relu_kernel(
             nc.scalar.activation(
                 dh_rows[:], dh_ps[:].rearrange("s (m t) -> s t m", t=PACK), ACT.Copy, scale=gate_cols[:, e : e + 1]
             )
-            turned[e] = ps_turn.tile([P, PACK, C], F32, name="turned")
+            turned[e] = ps_turn.tile([P, PACK, C], F32, name="turned", tag=f"turn{e % 3}")
             for t in range(PACK):
                 nc.tensor.transpose(turned[e][:, t, :], dh_rows[:, t, :], ident[:])
 
@@ -199,7 +200,10 @@ def tile_moe_bdx_glu_relu_kernel(
             )
 
         def second_product(e):
-            dx_ps = ps_dx.tile([P, C], F32, name="dx_ps")
+            if e == 3:
+                dx_ps = ps_turn.tile([P, C], F32, name="dx_ps", tag=f"turn{(e + 1) % 3}")
+            else:
+                dx_ps = ps_dx.tile([P, C], F32, name="dx_ps")
             for j, weights in enumerate((w1_w, w3_w)):
                 nc.tensor.matmul_mx(
                     out=dx_ps[:],

@@ -22,10 +22,11 @@ ACT = mybir.ActivationFunctionType
 P = 128
 PACK = 4
 PASSES = N // (P * PACK)
-GROUPS = [(0, 2), (2, 4), (4, 6)]
+PAIRS = [(0, 2), (2, 4), (4, 6)]
+A3_PARTS = [(0, 2), (2, 4), (4, 5), (5, 6)]
+W13_PARTS = [(0, 4), (4, 6)]
 EARLY = 2 * PASSES
 FIRST_SLOTS = 2 * C
-SCATTERS = [(0, 256), (256, 512), (512, 768)]
 
 
 def tile_moe_bdx_glu_relu_kernel(
@@ -35,133 +36,117 @@ def tile_moe_bdx_glu_relu_kernel(
     with ExitStack() as ctx:
         keep = ctx.enter_context(tc.tile_pool(name="keep", bufs=1))
         ring = ctx.enter_context(tc.tile_pool(name="ring", bufs=3))
-        two = ctx.enter_context(tc.tile_pool(name="two", bufs=2))
         ps_dh = ctx.enter_context(tc.psum_pool(name="ps_dh", bufs=2))
-        ps_turn = ctx.enter_context(tc.psum_pool(name="ps_turn", bufs=1))
+        ps_turn = ctx.enter_context(tc.psum_pool(name="ps_turn", bufs=4))
         ps_dx = ctx.enter_context(tc.psum_pool(name="ps_dx", bufs=2))
-        ps_gate = ctx.enter_context(tc.psum_pool(name="ps_gate", bufs=1))
 
-        group_of = {e: g for g, (lo, hi) in enumerate(GROUPS) for e in range(lo, hi)}
-        widths = [hi - lo for lo, hi in GROUPS]
+        def place(parts, e):
+            return [(g, e - lo) for g, (lo, hi) in enumerate(parts) if lo <= e < hi][0]
 
         offsets = keep.tile([P, SLOTS // 16], U16, name="offsets")
         dy_w = [keep.tile([P, T], I32, name=f"dy_w{o}", align_bytes=64) for o in range(PASSES)]
         dy_s = keep.tile([P, PASSES, T], U8, name="dy_s", align_bytes=64)
-        w2_w = [keep.tile([P, w * PASSES, 2 * H], U8, name=f"w2_w{g}", align_bytes=64) for g, w in enumerate(widths)]
+        w2_w = [keep.tile([P, (hi - lo) * PASSES, 2 * H], U8, name=f"w2_w{lo}", align_bytes=64) for lo, hi in PAIRS]
         w2_s_early = keep.tile([P, EARLY, H], U8, name="w2_s_early", align_bytes=64)
         w2_s_late = keep.tile([P, E * PASSES - EARLY, H], U8, name="w2_s_late", align_bytes=64)
-        w1_w = keep.tile([P, E, 2 * K], U8, name="w1_w", align_bytes=64)
-        w3_w = keep.tile([P, E, 2 * K], U8, name="w3_w", align_bytes=64)
-        w13_s = keep.tile([P, 2, E, K], U8, name="w13_s", align_bytes=64)
-        a1_t = [keep.tile([P, PACK, w * C], F32, name=f"a1_t{g}") for g, w in enumerate(widths)]
-        a3_t = [keep.tile([P, PACK, w * C], F32, name=f"a3_t{g}") for g, w in enumerate(widths)]
+        w1_w = [keep.tile([P, hi - lo, 2 * K], U8, name=f"w1_w{lo}", align_bytes=64) for lo, hi in W13_PARTS]
+        w3_w = [keep.tile([P, hi - lo, 2 * K], U8, name=f"w3_w{lo}", align_bytes=64) for lo, hi in W13_PARTS]
+        w1_s = keep.tile([P, E, K], U8, name="w1_s", align_bytes=64)
+        w3_s = keep.tile([P, E, K], U8, name="w3_s", align_bytes=64)
+        a1_t = [keep.tile([P, PACK, (hi - lo) * C], F32, name=f"a1_t{lo}") for lo, hi in PAIRS]
+        a3_t = [keep.tile([P, PACK, (hi - lo) * C], F32, name=f"a3_t{lo}") for lo, hi in A3_PARTS]
         codes = [keep.tile([P, 2, C], U32, name=f"codes{e}", align_bytes=64) for e in range(E)]
         scales = [keep.tile([P, 2, C], U8, name=f"scales{e}", align_bytes=64) for e in range(E)]
         gate_rows = keep.tile([P, C], F32, name="gate_rows")
         gate_cols = keep.tile([P, E], F32, name="gate_cols")
         ident = keep.tile([P, P], F32, name="ident")
+        zeros = keep.tile([P, C], F32, name="zeros")
         g_w = [keep.tile([P, SLOTS], U32, name=f"g_w{o}", align_bytes=64) for o in range(PASSES)]
         g_s = [keep.tile([P, SLOTS], U8, name=f"g_s{o}", align_bytes=64) for o in range(PASSES)]
         dx = keep.tile([P, SLOTS], F32, name="dx")
         result = keep.tile([P, T], F32, name="result")
 
-        def zero(flat):
-            nc.vector.memset(flat.bitcast(I32), 0)
+        def zero(plane):
+            nc.vector.memset(plane[:].rearrange("p a i -> p (a i)").bitcast(I32), 0)
 
-        zero_col = keep.tile([P, 1], F32, name="zero_col")
-        zero(dy_s[:, 0, :])
-        nc.gpsimd.memset(dy_s[:, 1, :].bitcast(I32), 0)
-        nc.vector.memset(zero_col[:], 0.0)
-        zero(w2_s_early[:].rearrange("p a i -> p (a i)"))
-        zero(w2_s_late[:].rearrange("p a i -> p (a i)"))
-        zero(w13_s[:].rearrange("p j e k -> p (j e k)"))
-        nc.scalar.activation(result[:], zero_col[:].to_broadcast([P, T]), ACT.Copy)
+        zero(dy_s)
+        nc.vector.memset(zeros[:], 0.0)
+        for plane in (w2_s_early, w2_s_late, w1_s, w3_s):
+            zero(plane)
         nc.gpsimd.memset(gate_rows[:], 0.0)
-        nc.gpsimd.dma_start(out=gate_rows[0:E, :], in_=gate[0].rearrange("(e c) -> e c", c=C))
+        nc.scalar.dma_start(out=gate_rows[0:E, :], in_=gate[0].rearrange("(e c) -> e c", c=C))
+        nc.scalar.activation(result[:], zeros[:, 0:1].to_broadcast([P, T]), ACT.Copy)
         make_identity(nc, ident[:])
 
-        def load_scale_rows(queue, plane, scales_by_r, r):
-            queue.dma_start(out=plane[r:P:32].bitcast(I32), in_=scales_by_r[r].bitcast(I32))
+        def load_scale_rows(plane, rows):
+            by_r = rows.rearrange("a (q r) i -> r q a i", r=4)
+            for r in range(4):
+                nc.sync.dma_start(out=plane[r:P:32].bitcast(I32), in_=by_r[r].bitcast(I32))
 
-        w2_s_by_r = w2_scales.rearrange("e s (q r) i -> r q (e s) i", r=4)
-        w1_s_by_r = w1_scales.rearrange("e s (q r) k -> r q (e s) k", r=4)
-        w3_s_by_r = w3_scales.rearrange("e s (q r) k -> r q (e s) k", r=4)
-        a1_v = a1.rearrange("(p t) s -> p t s", t=PACK)
-        a3_v = a3.rearrange("(p t) s -> p t s", t=PACK)
-        w2_v = w2_words.rearrange("e s p b -> p (e s) b")
+        def load_words(tile, words, lo, hi):
+            nc.sync.dma_start(out=tile[:].bitcast(I32), in_=words[lo:hi].rearrange("e s p b -> p (e s) b").bitcast(I32))
 
-        dy_s_by_r = dy_scales.rearrange("o (q r) t -> r q o t", r=4)
+        def load_saved(tile, saved, lo, hi):
+            nc.sync.dma_start(out=tile[:], in_=saved.rearrange("(p t) s -> p t s", t=PACK)[:, :, lo * C : hi * C])
 
-        def load_dy_words(o):
-            nc.sync.dma_start(out=dy_w[o][:], in_=dy_words[o].rearrange("p t d -> p (t d)").bitcast(I32))
+        w2_rows = w2_scales.rearrange("e s f i -> (e s) f i")
 
         nc.sync.dma_start(offsets[:], offs)
-        for r in range(4):
-            load_scale_rows(nc.sync, dy_s, dy_s_by_r, r)
-        load_dy_words(0)
-        load_dy_words(1)
-        for r in range(4):
-            load_scale_rows(nc.gpsimd, w2_s_late, w2_s_by_r[:, :, EARLY:], r)
+        for o in range(PASSES):
+            nc.sync.dma_start(out=dy_w[o][:], in_=dy_words[o].rearrange("p t d -> p (t d)").bitcast(I32))
+        load_scale_rows(dy_s, dy_scales)
+        load_words(w2_w[0], w2_words, *PAIRS[0])
+        load_scale_rows(w2_s_early, w2_rows[:EARLY])
+        load_saved(a1_t[0], a1, *PAIRS[0])
+        load_saved(a3_t[0], a3, *A3_PARTS[0])
+        load_words(w2_w[1], w2_words, *PAIRS[1])
+        load_scale_rows(w2_s_late, w2_rows[EARLY:])
+        load_saved(a1_t[1], a1, *PAIRS[1])
+        load_saved(a3_t[1], a3, *A3_PARTS[1])
+        load_words(w2_w[2], w2_words, *PAIRS[2])
+        load_scale_rows(w1_s, w1_scales.rearrange("e s f k -> (e s) f k"))
+        load_saved(a1_t[2], a1, *PAIRS[2])
+        load_scale_rows(w3_s, w3_scales.rearrange("e s f k -> (e s) f k"))
+        load_words(w1_w[0], w1_words, *W13_PARTS[0])
+        load_words(w3_w[0], w3_words, *W13_PARTS[0])
+        load_saved(a3_t[2], a3, *A3_PARTS[2])
+        load_saved(a3_t[3], a3, *A3_PARTS[3])
+        load_words(w1_w[1], w1_words, *W13_PARTS[1])
+        load_words(w3_w[1], w3_words, *W13_PARTS[1])
 
-        def load_w2(g):
-            lo, hi = GROUPS[g]
-            nc.sync.dma_start(out=w2_w[g][:].bitcast(I32), in_=w2_v[:, lo * PASSES : hi * PASSES, :].bitcast(I32))
-
-        def load_saved(tiles, view, g):
-            lo, hi = GROUPS[g]
-            nc.sync.dma_start(out=tiles[g][:], in_=view[:, :, lo * C : hi * C])
-
-        for g in range(len(GROUPS)):
-            if g == len(GROUPS) - 1:
-                for tile, words in ((w1_w, w1_words), (w3_w, w3_words)):
-                    nc.sync.dma_start(out=tile[:].bitcast(I32), in_=words.rearrange("e s p b -> p (e s) b").bitcast(I32))
-            load_w2(g)
-            if g == 0:
-                for r in range(4):
-                    load_scale_rows(nc.sync, w2_s_early, w2_s_by_r[:, :, :EARLY], r)
-            load_saved(a1_t, a1_v, g)
-            load_saved(a3_t, a3_v, g)
-        for r in range(4):
-            load_scale_rows(nc.gpsimd, w13_s[:, 0], w1_s_by_r, r)
-            load_scale_rows(nc.gpsimd, w13_s[:, 1], w3_s_by_r, r)
-
-        gate_ps = ps_gate.tile([P, P], F32, name="gate_ps")
+        gate_ps = ps_dx.tile([P, P], F32, name="dx_ps")
         nc.tensor.transpose(gate_ps[:], gate_rows[:], ident[:])
         nc.scalar.activation(gate_cols[:], gate_ps[:, 0:E], ACT.Copy)
 
-        def gather_words(o, lo, hi):
-            nc.vector.tensor_copy(g_w[o][:, lo:hi], dy_w[o][:].bitcast(U32).indirect(offsets[:, lo // 16 : hi // 16]))
-
-        def gather_scales(o, lo, hi):
-            nc.vector.tensor_copy(g_s[o][:, lo:hi], dy_s[:, o, :].indirect(offsets[:, lo // 16 : hi // 16]))
+        def listed(lo, hi):
+            return offsets[:, lo // 16 : hi // 16]
 
         for o in range(PASSES):
-            gather_scales(o, 0, SLOTS)
+            nc.vector.tensor_copy(g_w[o][:], dy_w[o][:].bitcast(U32).indirect(offsets[:]))
         for lo, hi in ((0, FIRST_SLOTS), (FIRST_SLOTS, SLOTS)):
             for o in range(PASSES):
-                gather_words(o, lo, hi)
+                nc.vector.tensor_copy(g_s[o][:, lo:hi], dy_s[:, o, :].indirect(listed(lo, hi)))
 
         turned = {}
         masked = {}
-        relu = {}
         da = {}
 
-        def local(e):
-            return e - GROUPS[group_of[e]][0]
-
-        def w2_scale_plane(a):
-            return w2_s_early[:, a, :] if a < EARLY else w2_s_late[:, a - EARLY, :]
+        def saved_columns(tiles, parts, e):
+            g, j = place(parts, e)
+            return tiles[g][:, :, j * C : (j + 1) * C]
 
         def first_product(e):
             slots = slice(e * C, (e + 1) * C)
+            g, j = place(PAIRS, e)
             dh_ps = ps_dh.tile([P, H], F32, name="dh_ps")
             for o in range(PASSES):
+                a = e * PASSES + o
                 nc.tensor.matmul_mx(
                     out=dh_ps[:],
                     lhsT=g_w[o][:, slots].bitcast(FP8X4),
                     lhsT_scale=g_s[o][:, slots],
-                    rhs=w2_w[group_of[e]][:, local(e) * PASSES + o, :].bitcast(FP4X4),
-                    rhs_scale=w2_scale_plane(e * PASSES + o),
+                    rhs=w2_w[g][:, j * PASSES + o, :].bitcast(FP4X4),
+                    rhs_scale=w2_s_early[:, a, :] if a < EARLY else w2_s_late[:, a - EARLY, :],
                     start=(o == 0),
                     stop=(o == PASSES - 1),
                 )
@@ -169,28 +154,24 @@ def tile_moe_bdx_glu_relu_kernel(
             nc.scalar.activation(
                 dh_rows[:], dh_ps[:].rearrange("s (m t) -> s t m", t=PACK), ACT.Copy, scale=gate_cols[:, e : e + 1]
             )
-            turned[e] = ps_turn.tile([P, PACK, C], F32, name="turned", tag=f"turn{e % 3}")
+            turned[e] = ps_turn.tile([P, PACK, C], F32, name="turned")
             for t in range(PACK):
                 nc.tensor.transpose(turned[e][:, t, :], dh_rows[:, t, :], ident[:])
 
-        def masked_a3(g):
-            masked[g] = two.tile([P, PACK, widths[g] * C], F32, name="masked")
-            nc.vector.scalar_tensor_tensor(masked[g][:], a1_t[g][:], 0.0, a3_t[g][:], ALU.is_gt, ALU.mult)
-
-        def relu_a1(e):
-            relu[e] = ring.tile([P, PACK, C], F32, name="relu")
-            nc.scalar.activation(relu[e][:], a1_t[group_of[e]][:, :, local(e) * C : (local(e) + 1) * C], ACT.Relu)
+        def mask_dh(e):
+            masked[e] = ring.tile([P, PACK, C], F32, name="masked")
+            nc.vector.scalar_tensor_tensor(
+                masked[e][:], saved_columns(a1_t, PAIRS, e), 0.0, turned[e][:], ALU.is_gt, ALU.mult
+            )
+            da[e] = ring.tile([P, 2, C, PACK], BF16, name="da", align_bytes=64)
 
         def by_pairs(planes):
             return planes.rearrange("p t (c i) -> p c t i", i=2)
 
-        def gradients(e):
-            da[e] = ring.tile([P, 2, C, PACK], BF16, name="da", align_bytes=64)
-            cols = slice(local(e) * C, (local(e) + 1) * C)
-            for j, factor in enumerate((masked[group_of[e]][:, :, cols], relu[e][:])):
-                nc.vector.tensor_tensor(
-                    da[e][:, j].rearrange("p (c i) t -> p c t i", i=2), by_pairs(turned[e][:]), by_pairs(factor), ALU.mult
-                )
+        def gradient(e, j, factor):
+            nc.vector.tensor_tensor(
+                da[e][:, j].rearrange("p (c i) t -> p c t i", i=2), by_pairs(masked[e][:]), by_pairs(factor), ALU.mult
+            )
 
         def quantise(e):
             nc.vector.quantize_mx(
@@ -200,15 +181,13 @@ def tile_moe_bdx_glu_relu_kernel(
             )
 
         def second_product(e):
-            if e == 3:
-                dx_ps = ps_turn.tile([P, C], F32, name="dx_ps", tag=f"turn{(e + 1) % 3}")
-            else:
-                dx_ps = ps_dx.tile([P, C], F32, name="dx_ps")
-            for j, weights in enumerate((w1_w, w3_w)):
+            g, i = place(W13_PARTS, e)
+            dx_ps = ps_dx.tile([P, C], F32, name="dx_ps")
+            for j, (words, plane) in enumerate(((w1_w, w1_s), (w3_w, w3_s))):
                 nc.tensor.matmul_mx(
                     out=dx_ps[:],
-                    lhsT=weights[:, e, :].bitcast(FP4X4),
-                    lhsT_scale=w13_s[:, j, e, :],
+                    lhsT=words[g][:, i, :].bitcast(FP4X4),
+                    lhsT_scale=plane[:, e, :],
                     rhs=codes[e][:, j, :].bitcast(FP8X4),
                     rhs_scale=scales[e][:, j, :],
                     start=(j == 0),
@@ -216,27 +195,24 @@ def tile_moe_bdx_glu_relu_kernel(
                 )
             nc.scalar.copy(dx[:, e * C : (e + 1) * C], dx_ps[:])
 
-        def scatter(lo, hi):
-            nc.vector.tensor_copy(result[:].indirect(offsets[:, lo // 16 : hi // 16]), dx[:, lo:hi])
-
-        first_product(0)
-        relu_a1(0)
-        first_product(1)
-        for e in range(E):
-            if local(e) == 0:
-                masked_a3(group_of[e])
-            if e + 1 < E:
-                relu_a1(e + 1)
-            if e + 2 < E:
-                first_product(e + 2)
-            gradients(e)
-            if e > 0:
-                quantise(e - 1)
-                second_product(e - 1)
-            if e == 3:
-                scatter(*SCATTERS[0])
-        quantise(E - 1)
-        second_product(E - 1)
-        for lo, hi in SCATTERS[1:]:
-            scatter(lo, hi)
+        for lo, hi in PAIRS:
+            for e in range(lo, hi):
+                first_product(e)
+            for e in range(lo, hi):
+                mask_dh(e)
+            for e in range(lo, hi):
+                gradient(e, 1, saved_columns(a1_t, PAIRS, e))
+            for e in range(lo, hi):
+                gradient(e, 0, saved_columns(a3_t, A3_PARTS, e))
+            for e in range(lo, hi):
+                quantise(e)
+        for lo, hi in PAIRS[:-1]:
+            for e in range(lo, hi):
+                second_product(e)
+            nc.scalar.activation(result[:].indirect(listed(lo * C, hi * C)), dx[:, lo * C : hi * C], ACT.Copy)
+        for e in range(*PAIRS[-1]):
+            second_product(e)
+            nc.vector.tensor_tensor(
+                result[:].indirect(listed(e * C, (e + 1) * C)), dx[:, e * C : (e + 1) * C], zeros[:], ALU.add
+            )
         nc.sync.dma_start(out=out, in_=result[:])

@@ -24,7 +24,6 @@ PACK = 4
 PASSES = N // (P * PACK)
 PAIRS = [(0, 2), (2, 4), (4, 6)]
 A3_PARTS = [(0, 2), (2, 4), (4, 5), (5, 6)]
-W13_PARTS = [(0, 4), (4, 6)]
 EARLY = 2 * PASSES
 FIRST_SLOTS = 2 * C
 
@@ -49,12 +48,12 @@ def tile_moe_bdx_glu_relu_kernel(
         w2_w = [keep.tile([P, (hi - lo) * PASSES, 2 * H], U8, name=f"w2_w{lo}", align_bytes=64) for lo, hi in PAIRS]
         w2_s_early = keep.tile([P, EARLY, H], U8, name="w2_s_early", align_bytes=64)
         w2_s_late = keep.tile([P, E * PASSES - EARLY, H], U8, name="w2_s_late", align_bytes=64)
-        w1_w = [keep.tile([P, hi - lo, 2 * K], U8, name=f"w1_w{lo}", align_bytes=64) for lo, hi in W13_PARTS]
-        w3_w = [keep.tile([P, hi - lo, 2 * K], U8, name=f"w3_w{lo}", align_bytes=64) for lo, hi in W13_PARTS]
+        w1_w = [keep.tile([P, hi - lo, 2 * K], U8, name=f"w1_w{lo}", align_bytes=64) for lo, hi in PAIRS]
+        w3_w = [keep.tile([P, hi - lo, 2 * K], U8, name=f"w3_w{lo}", align_bytes=64) for lo, hi in PAIRS]
         w1_s = keep.tile([P, E, K], U8, name="w1_s", align_bytes=64)
         w3_s = keep.tile([P, E, K], U8, name="w3_s", align_bytes=64)
         a1_t = [keep.tile([P, PACK, (hi - lo) * C], F32, name=f"a1_t{lo}") for lo, hi in PAIRS]
-        a3_t = [keep.tile([P, PACK, (hi - lo) * C], F32, name=f"a3_t{lo}") for lo, hi in A3_PARTS]
+        a3_t = [keep.tile([P, PACK, (hi - lo) * C], F32, name=f"a3_t{lo}", tag=f"a3_t{lo}") for lo, hi in A3_PARTS]
         codes = [keep.tile([P, 2, C], U32, name=f"codes{e}", align_bytes=64) for e in range(E)]
         scales = [keep.tile([P, 2, C], U8, name=f"scales{e}", align_bytes=64) for e in range(E)]
         gate_rows = keep.tile([P, C], F32, name="gate_rows")
@@ -63,7 +62,7 @@ def tile_moe_bdx_glu_relu_kernel(
         zeros = keep.tile([P, C], F32, name="zeros")
         g_w = [keep.tile([P, SLOTS], U32, name=f"g_w{o}", align_bytes=64) for o in range(PASSES)]
         g_s = [keep.tile([P, SLOTS], U8, name=f"g_s{o}", align_bytes=64) for o in range(PASSES)]
-        dx = keep.tile([P, SLOTS], F32, name="dx")
+        dx = keep.tile([P, SLOTS - 2 * C], F32, name="dx")
         result = keep.tile([P, T], F32, name="result")
 
         def zero(plane):
@@ -71,8 +70,6 @@ def tile_moe_bdx_glu_relu_kernel(
 
         zero(dy_s)
         nc.vector.memset(zeros[:], 0.0)
-        for plane in (w2_s_early, w2_s_late, w1_s, w3_s):
-            zero(plane)
         nc.gpsimd.memset(gate_rows[:], 0.0)
         nc.scalar.dma_start(out=gate_rows[0:E, :], in_=gate[0].rearrange("(e c) -> e c", c=C))
         nc.scalar.activation(result[:], zeros[:, 0:1].to_broadcast([P, T]), ACT.Copy)
@@ -102,17 +99,19 @@ def tile_moe_bdx_glu_relu_kernel(
         load_words(w2_w[1], w2_words, *PAIRS[1])
         load_scale_rows(w2_s_late, w2_rows[EARLY:])
         load_saved(a1_t[1], a1, *PAIRS[1])
-        load_saved(a3_t[1], a3, *A3_PARTS[1])
         load_words(w2_w[2], w2_words, *PAIRS[2])
         load_scale_rows(w1_s, w1_scales.rearrange("e s f k -> (e s) f k"))
-        load_saved(a1_t[2], a1, *PAIRS[2])
+        load_saved(a3_t[1], a3, *A3_PARTS[1])
         load_scale_rows(w3_s, w3_scales.rearrange("e s f k -> (e s) f k"))
-        load_words(w1_w[0], w1_words, *W13_PARTS[0])
-        load_words(w3_w[0], w3_words, *W13_PARTS[0])
+        load_words(w1_w[0], w1_words, *PAIRS[0])
+        load_words(w3_w[0], w3_words, *PAIRS[0])
+        load_saved(a1_t[2], a1, *PAIRS[2])
+        load_words(w1_w[1], w1_words, *PAIRS[1])
+        load_words(w3_w[1], w3_words, *PAIRS[1])
         load_saved(a3_t[2], a3, *A3_PARTS[2])
+        load_words(w1_w[2], w1_words, *PAIRS[2])
+        load_words(w3_w[2], w3_words, *PAIRS[2])
         load_saved(a3_t[3], a3, *A3_PARTS[3])
-        load_words(w1_w[1], w1_words, *W13_PARTS[1])
-        load_words(w3_w[1], w3_words, *W13_PARTS[1])
 
         gate_ps = ps_dx.tile([P, P], F32, name="dx_ps")
         nc.tensor.transpose(gate_ps[:], gate_rows[:], ident[:])
@@ -180,8 +179,8 @@ def tile_moe_bdx_glu_relu_kernel(
                 in_=da[e][:].rearrange("p j s t -> p (j s t)"),
             )
 
-        def second_product(e):
-            g, i = place(W13_PARTS, e)
+        def second_product(e, columns):
+            g, i = place(PAIRS, e)
             dx_ps = ps_dx.tile([P, C], F32, name="dx_ps")
             for j, (words, plane) in enumerate(((w1_w, w1_s), (w3_w, w3_s))):
                 nc.tensor.matmul_mx(
@@ -193,26 +192,35 @@ def tile_moe_bdx_glu_relu_kernel(
                     start=(j == 0),
                     stop=(j == 1),
                 )
-            nc.scalar.copy(dx[:, e * C : (e + 1) * C], dx_ps[:])
+            nc.scalar.copy(columns, dx_ps[:])
+
+        def da3(e):
+            gradient(e, 1, saved_columns(a1_t, PAIRS, e))
+
+        def da1(e):
+            gradient(e, 0, saved_columns(a3_t, A3_PARTS, e))
 
         for lo, hi in PAIRS:
             for e in range(lo, hi):
                 first_product(e)
             for e in range(lo, hi):
                 mask_dh(e)
-            for e in range(lo, hi):
-                gradient(e, 1, saved_columns(a1_t, PAIRS, e))
-            for e in range(lo, hi):
-                gradient(e, 0, saved_columns(a3_t, A3_PARTS, e))
-            for e in range(lo, hi):
-                quantise(e)
+            if hi < E:
+                for step in (da3, da1, quantise):
+                    for e in range(lo, hi):
+                        step(e)
+        da3(E - 2)
+        da1(E - 2)
+        da3(E - 1)
+        quantise(E - 2)
+        da1(E - 1)
+        quantise(E - 1)
         for lo, hi in PAIRS[:-1]:
             for e in range(lo, hi):
-                second_product(e)
+                second_product(e, dx[:, e * C : (e + 1) * C])
             nc.scalar.activation(result[:].indirect(listed(lo * C, hi * C)), dx[:, lo * C : hi * C], ACT.Copy)
-        for e in range(*PAIRS[-1]):
-            second_product(e)
-            nc.vector.tensor_tensor(
-                result[:].indirect(listed(e * C, (e + 1) * C)), dx[:, e * C : (e + 1) * C], zeros[:], ALU.add
-            )
+        for e, tag in ((E - 2, f"a3_t{E - 1}"), (E - 1, "dx_last")):
+            dx_one = keep.tile([P, C], F32, name=f"dx{e}", tag=tag)
+            second_product(e, dx_one[:])
+            nc.vector.tensor_tensor(result[:].indirect(listed(e * C, (e + 1) * C)), dx_one[:], zeros[:], ALU.add)
         nc.sync.dma_start(out=out, in_=result[:])

@@ -1,7 +1,6 @@
 from contextlib import ExitStack
 
 import concourse.mybir as mybir
-from concourse.masks import make_identity
 
 K, T, E, C, H, N = 128, 1536, 6, 128, 512, 1024
 SLOTS = E * C
@@ -23,8 +22,8 @@ P = 128
 PACK = 4
 PASSES = N // (P * PACK)
 PAIRS = [(0, 2), (2, 4), (4, 6)]
+W2_PARTS = [(0, 1), (1, 2), (2, 4), (4, 6)]
 A3_PARTS = [(0, 2), (2, 4), (4, 5), (5, 6)]
-EARLY = 2 * PASSES
 FIRST_SLOTS = 2 * C
 
 
@@ -45,9 +44,8 @@ def tile_moe_bdx_glu_relu_kernel(
         offsets = keep.tile([P, SLOTS // 16], U16, name="offsets")
         dy_w = [keep.tile([P, T], I32, name=f"dy_w{o}", align_bytes=64) for o in range(PASSES)]
         dy_s = keep.tile([P, PASSES, T], U8, name="dy_s", align_bytes=64)
-        w2_w = [keep.tile([P, (hi - lo) * PASSES, 2 * H], U8, name=f"w2_w{lo}", align_bytes=64) for lo, hi in PAIRS]
-        w2_s_early = keep.tile([P, EARLY, H], U8, name="w2_s_early", align_bytes=64)
-        w2_s_late = keep.tile([P, E * PASSES - EARLY, H], U8, name="w2_s_late", align_bytes=64)
+        w2_w = [keep.tile([P, (hi - lo) * PASSES, 2 * H], U8, name=f"w2_w{lo}", align_bytes=64) for lo, hi in W2_PARTS]
+        w2_s = [keep.tile([P, 2 * PASSES, H], U8, name=f"w2_s{lo}", align_bytes=64) for lo, hi in PAIRS[:-1]]
         w1_w = [keep.tile([P, hi - lo, 2 * K], U8, name=f"w1_w{lo}", align_bytes=64) for lo, hi in PAIRS]
         w3_w = [keep.tile([P, hi - lo, 2 * K], U8, name=f"w3_w{lo}", align_bytes=64) for lo, hi in PAIRS]
         w1_s = keep.tile([P, E, K], U8, name="w1_s", align_bytes=64)
@@ -73,12 +71,17 @@ def tile_moe_bdx_glu_relu_kernel(
         nc.gpsimd.memset(gate_rows[:], 0.0)
         nc.scalar.dma_start(out=gate_rows[0:E, :], in_=gate[0].rearrange("(e c) -> e c", c=C))
         nc.scalar.activation(result[:], zeros[:, 0:1].to_broadcast([P, T]), ACT.Copy)
-        make_identity(nc, ident[:])
+        blank = keep.tile([P, P], F32, name="blank", tag="reused", align_bytes=64)
+        nc.gpsimd.memset(blank[:], 0.0)
+        nc.gpsimd.affine_select(
+            out=ident[:], in_=blank[:], compare_op=ALU.not_equal, fill=1.0, base=0, pattern=[[-1, P]], channel_multiplier=1
+        )
+        w2_s.append(keep.tile([P, 2 * PASSES, H], U8, name="w2_s_last", tag="reused", align_bytes=64))
 
-        def load_scale_rows(plane, rows):
+        def load_scale_rows(plane, rows, queue=nc.sync):
             by_r = rows.rearrange("a (q r) i -> r q a i", r=4)
             for r in range(4):
-                nc.sync.dma_start(out=plane[r:P:32].bitcast(I32), in_=by_r[r].bitcast(I32))
+                queue.dma_start(out=plane[r:P:32].bitcast(I32), in_=by_r[r].bitcast(I32))
 
         def load_words(tile, words, lo, hi):
             nc.sync.dma_start(out=tile[:].bitcast(I32), in_=words[lo:hi].rearrange("e s p b -> p (e s) b").bitcast(I32))
@@ -86,29 +89,32 @@ def tile_moe_bdx_glu_relu_kernel(
         def load_saved(tile, saved, lo, hi):
             nc.sync.dma_start(out=tile[:], in_=saved.rearrange("(p t) s -> p t s", t=PACK)[:, :, lo * C : hi * C])
 
-        w2_rows = w2_scales.rearrange("e s f i -> (e s) f i")
+        def w2_rows(lo, hi):
+            return w2_scales[lo:hi].rearrange("e s f i -> (e s) f i")
 
+        load_scale_rows(w2_s[2], w2_rows(*PAIRS[2]), nc.gpsimd)
         nc.sync.dma_start(offsets[:], offs)
         for o in range(PASSES):
             nc.sync.dma_start(out=dy_w[o][:], in_=dy_words[o].rearrange("p t d -> p (t d)").bitcast(I32))
         load_scale_rows(dy_s, dy_scales)
-        load_words(w2_w[0], w2_words, *PAIRS[0])
-        load_scale_rows(w2_s_early, w2_rows[:EARLY])
+        load_words(w2_w[0], w2_words, *W2_PARTS[0])
+        load_scale_rows(w2_s[0], w2_rows(*PAIRS[0]))
+        load_words(w2_w[1], w2_words, *W2_PARTS[1])
         load_saved(a1_t[0], a1, *PAIRS[0])
+        load_words(w2_w[2], w2_words, *W2_PARTS[2])
+        load_scale_rows(w2_s[1], w2_rows(*PAIRS[1]))
         load_saved(a3_t[0], a3, *A3_PARTS[0])
-        load_words(w2_w[1], w2_words, *PAIRS[1])
-        load_scale_rows(w2_s_late, w2_rows[EARLY:])
         load_saved(a1_t[1], a1, *PAIRS[1])
-        load_words(w2_w[2], w2_words, *PAIRS[2])
+        load_words(w2_w[3], w2_words, *W2_PARTS[3])
         load_scale_rows(w1_s, w1_scales.rearrange("e s f k -> (e s) f k"))
         load_saved(a3_t[1], a3, *A3_PARTS[1])
         load_scale_rows(w3_s, w3_scales.rearrange("e s f k -> (e s) f k"))
         load_words(w1_w[0], w1_words, *PAIRS[0])
         load_words(w3_w[0], w3_words, *PAIRS[0])
         load_saved(a1_t[2], a1, *PAIRS[2])
+        load_saved(a3_t[2], a3, *A3_PARTS[2])
         load_words(w1_w[1], w1_words, *PAIRS[1])
         load_words(w3_w[1], w3_words, *PAIRS[1])
-        load_saved(a3_t[2], a3, *A3_PARTS[2])
         load_words(w1_w[2], w1_words, *PAIRS[2])
         load_words(w3_w[2], w3_words, *PAIRS[2])
         load_saved(a3_t[3], a3, *A3_PARTS[3])
@@ -136,16 +142,15 @@ def tile_moe_bdx_glu_relu_kernel(
 
         def first_product(e):
             slots = slice(e * C, (e + 1) * C)
-            g, j = place(PAIRS, e)
+            g, j = place(W2_PARTS, e)
             dh_ps = ps_dh.tile([P, H], F32, name="dh_ps")
             for o in range(PASSES):
-                a = e * PASSES + o
                 nc.tensor.matmul_mx(
                     out=dh_ps[:],
                     lhsT=g_w[o][:, slots].bitcast(FP8X4),
                     lhsT_scale=g_s[o][:, slots],
                     rhs=w2_w[g][:, j * PASSES + o, :].bitcast(FP4X4),
-                    rhs_scale=w2_s_early[:, a, :] if a < EARLY else w2_s_late[:, a - EARLY, :],
+                    rhs_scale=w2_s[e // 2][:, e % 2 * PASSES + o, :],
                     start=(o == 0),
                     stop=(o == PASSES - 1),
                 )

@@ -34,9 +34,8 @@ def tile_moe_bdx_glu_relu_kernel(
     with ExitStack() as ctx:
         keep = ctx.enter_context(tc.tile_pool(name="keep", bufs=1))
         ring = ctx.enter_context(tc.tile_pool(name="ring", bufs=3))
-        ps_dh = ctx.enter_context(tc.psum_pool(name="ps_dh", bufs=2))
-        ps_turn = ctx.enter_context(tc.psum_pool(name="ps_turn", bufs=4))
-        ps_dx = ctx.enter_context(tc.psum_pool(name="ps_dx", bufs=2))
+        ps_sum = ctx.enter_context(tc.psum_pool(name="ps_sum", bufs=2))
+        ps_turn = ctx.enter_context(tc.psum_pool(name="ps_turn", bufs=E))
 
         def place(parts, e):
             return [(g, e - lo) for g, (lo, hi) in enumerate(parts) if lo <= e < hi][0]
@@ -48,8 +47,10 @@ def tile_moe_bdx_glu_relu_kernel(
         w2_s = [keep.tile([P, 2 * PASSES, H], U8, name=f"w2_s{lo}", align_bytes=64) for lo, hi in PAIRS[:-1]]
         w1_w = [keep.tile([P, hi - lo, 2 * K], U8, name=f"w1_w{lo}", align_bytes=64) for lo, hi in PAIRS]
         w3_w = [keep.tile([P, hi - lo, 2 * K], U8, name=f"w3_w{lo}", align_bytes=64) for lo, hi in PAIRS]
-        w1_s = keep.tile([P, E, K], U8, name="w1_s", align_bytes=64)
-        w3_s = keep.tile([P, E, K], U8, name="w3_s", align_bytes=64)
+        late_s = keep.tile([P, 2 * PASSES * H + 2 * E * K], U8, name="late_s", align_bytes=64)
+        w2_s_last = late_s[:, 0 : 2 * PASSES * H].rearrange("p (a i) -> p a i", i=H)
+        w1_s = late_s[:, 2 * PASSES * H : 2 * PASSES * H + E * K].rearrange("p (e k) -> p e k", k=K)
+        w3_s = late_s[:, 2 * PASSES * H + E * K :].rearrange("p (e k) -> p e k", k=K)
         a1_t = [keep.tile([P, PACK, (hi - lo) * C], F32, name=f"a1_t{lo}") for lo, hi in PAIRS]
         a3_t = [keep.tile([P, PACK, (hi - lo) * C], F32, name=f"a3_t{lo}", tag=f"a3_t{lo}") for lo, hi in A3_PARTS]
         codes = [keep.tile([P, 2, C], U32, name=f"codes{e}", align_bytes=64) for e in range(E)]
@@ -71,17 +72,23 @@ def tile_moe_bdx_glu_relu_kernel(
         nc.gpsimd.memset(gate_rows[:], 0.0)
         nc.scalar.dma_start(out=gate_rows[0:E, :], in_=gate[0].rearrange("(e c) -> e c", c=C))
         nc.scalar.activation(result[:], zeros[:, 0:1].to_broadcast([P, T]), ACT.Copy)
-        blank = keep.tile([P, P], F32, name="blank", tag="reused", align_bytes=64)
-        nc.gpsimd.memset(blank[:], 0.0)
+        nc.gpsimd.memset(ident[:], 0.0)
         nc.gpsimd.affine_select(
-            out=ident[:], in_=blank[:], compare_op=ALU.not_equal, fill=1.0, base=0, pattern=[[-1, P]], channel_multiplier=1
+            out=ident[:], in_=ident[:], compare_op=ALU.not_equal, fill=1.0, base=0, pattern=[[-1, P]], channel_multiplier=1
         )
-        w2_s.append(keep.tile([P, 2 * PASSES, H], U8, name="w2_s_last", tag="reused", align_bytes=64))
+        w2_s.append(w2_s_last)
 
-        def load_scale_rows(plane, rows, queue=nc.sync):
+        def stage_scale_rows(plane, rows):
+            nc.sync.dma_start(out=plane[0:P:8].bitcast(I32), in_=rows.rearrange("a f i -> f a i").bitcast(I32))
+
+        def place_scale_rows(tile):
+            for r in range(1, 4):
+                nc.gpsimd.dma_start(out=tile[r:P:32, :].bitcast(I32), in_=tile[8 * r : P : 32, :].bitcast(I32))
+
+        def load_scale_rows(plane, rows):
             by_r = rows.rearrange("a (q r) i -> r q a i", r=4)
             for r in range(4):
-                queue.dma_start(out=plane[r:P:32].bitcast(I32), in_=by_r[r].bitcast(I32))
+                nc.sync.dma_start(out=plane[r:P:32].bitcast(I32), in_=by_r[r].bitcast(I32))
 
         def load_words(tile, words, lo, hi):
             nc.sync.dma_start(out=tile[:].bitcast(I32), in_=words[lo:hi].rearrange("e s p b -> p (e s) b").bitcast(I32))
@@ -92,12 +99,15 @@ def tile_moe_bdx_glu_relu_kernel(
         def w2_rows(lo, hi):
             return w2_scales[lo:hi].rearrange("e s f i -> (e s) f i")
 
-        load_scale_rows(w2_s[2], w2_rows(*PAIRS[2]), nc.gpsimd)
         nc.sync.dma_start(offsets[:], offs)
         for o in range(PASSES):
             nc.sync.dma_start(out=dy_w[o][:], in_=dy_words[o].rearrange("p t d -> p (t d)").bitcast(I32))
         load_scale_rows(dy_s, dy_scales)
         load_words(w2_w[0], w2_words, *W2_PARTS[0])
+        stage_scale_rows(w2_s_last, w2_rows(*PAIRS[2]))
+        stage_scale_rows(w1_s, w1_scales.rearrange("e s f k -> (e s) f k"))
+        stage_scale_rows(w3_s, w3_scales.rearrange("e s f k -> (e s) f k"))
+        place_scale_rows(late_s)
         load_scale_rows(w2_s[0], w2_rows(*PAIRS[0]))
         load_words(w2_w[1], w2_words, *W2_PARTS[1])
         load_saved(a1_t[0], a1, *PAIRS[0])
@@ -106,9 +116,7 @@ def tile_moe_bdx_glu_relu_kernel(
         load_saved(a3_t[0], a3, *A3_PARTS[0])
         load_saved(a1_t[1], a1, *PAIRS[1])
         load_words(w2_w[3], w2_words, *W2_PARTS[3])
-        load_scale_rows(w1_s, w1_scales.rearrange("e s f k -> (e s) f k"))
         load_saved(a3_t[1], a3, *A3_PARTS[1])
-        load_scale_rows(w3_s, w3_scales.rearrange("e s f k -> (e s) f k"))
         load_words(w1_w[0], w1_words, *PAIRS[0])
         load_words(w3_w[0], w3_words, *PAIRS[0])
         load_saved(a1_t[2], a1, *PAIRS[2])
@@ -119,7 +127,7 @@ def tile_moe_bdx_glu_relu_kernel(
         load_words(w3_w[2], w3_words, *PAIRS[2])
         load_saved(a3_t[3], a3, *A3_PARTS[3])
 
-        gate_ps = ps_dx.tile([P, P], F32, name="dx_ps")
+        gate_ps = ps_sum.tile([P, P], F32, name="gate_ps", tag="sum")
         nc.tensor.transpose(gate_ps[:], gate_rows[:], ident[:])
         nc.scalar.activation(gate_cols[:], gate_ps[:, 0:E], ACT.Copy)
 
@@ -143,7 +151,7 @@ def tile_moe_bdx_glu_relu_kernel(
         def first_product(e):
             slots = slice(e * C, (e + 1) * C)
             g, j = place(W2_PARTS, e)
-            dh_ps = ps_dh.tile([P, H], F32, name="dh_ps")
+            dh_ps = ps_sum.tile([P, H], F32, name="dh_ps", tag="sum")
             for o in range(PASSES):
                 nc.tensor.matmul_mx(
                     out=dh_ps[:],
@@ -186,7 +194,7 @@ def tile_moe_bdx_glu_relu_kernel(
 
         def second_product(e, columns):
             g, i = place(PAIRS, e)
-            dx_ps = ps_dx.tile([P, C], F32, name="dx_ps")
+            dx_ps = ps_sum.tile([P, C], F32, name="dx_ps", tag="sum")
             for j, (words, plane) in enumerate(((w1_w, w1_s), (w3_w, w3_s))):
                 nc.tensor.matmul_mx(
                     out=dx_ps[:],

@@ -22,6 +22,7 @@ P = 128
 PACK = 4
 PASSES = N // (P * PACK)
 PAIRS = [(0, 2), (2, 4), (4, 6)]
+W2_SCALE_PARTS = [(0, 2), (2, 6)]
 W2_PARTS = [(0, 1), (1, 2), (2, 4), (4, 6)]
 A3_PARTS = [(0, 2), (2, 4), (4, 5), (5, 6)]
 FIRST_SLOTS = 2 * C
@@ -44,13 +45,12 @@ def tile_moe_bdx_glu_relu_kernel(
         dy_w = [keep.tile([P, T], I32, name=f"dy_w{o}", align_bytes=64) for o in range(PASSES)]
         dy_s = keep.tile([P, PASSES, T], U8, name="dy_s", align_bytes=64)
         w2_w = [keep.tile([P, (hi - lo) * PASSES, 2 * H], U8, name=f"w2_w{lo}", align_bytes=64) for lo, hi in W2_PARTS]
-        w2_s = [keep.tile([P, 2 * PASSES, H], U8, name=f"w2_s{lo}", align_bytes=64) for lo, hi in PAIRS[:-1]]
+        w2_s = [keep.tile([P, (hi - lo) * PASSES, H], U8, name=f"w2_s{lo}", align_bytes=64) for lo, hi in W2_SCALE_PARTS]
         w1_w = [keep.tile([P, hi - lo, 2 * K], U8, name=f"w1_w{lo}", align_bytes=64) for lo, hi in PAIRS]
         w3_w = [keep.tile([P, hi - lo, 2 * K], U8, name=f"w3_w{lo}", align_bytes=64) for lo, hi in PAIRS]
-        late_s = keep.tile([P, 2 * PASSES * H + 2 * E * K], U8, name="late_s", align_bytes=64)
-        w2_s_last = late_s[:, 0 : 2 * PASSES * H].rearrange("p (a i) -> p a i", i=H)
-        w1_s = late_s[:, 2 * PASSES * H : 2 * PASSES * H + E * K].rearrange("p (e k) -> p e k", k=K)
-        w3_s = late_s[:, 2 * PASSES * H + E * K :].rearrange("p (e k) -> p e k", k=K)
+        late_s = keep.tile([P, 2 * E * K], U8, name="late_s", align_bytes=64)
+        w1_s = late_s[:, 0 : E * K].rearrange("p (e k) -> p e k", k=K)
+        w3_s = late_s[:, E * K :].rearrange("p (e k) -> p e k", k=K)
         a1_t = [keep.tile([P, PACK, (hi - lo) * C], F32, name=f"a1_t{lo}") for lo, hi in PAIRS]
         a3_t = [keep.tile([P, PACK, (hi - lo) * C], F32, name=f"a3_t{lo}", tag=f"a3_t{lo}") for lo, hi in A3_PARTS]
         codes = [keep.tile([P, 2, C], U32, name=f"codes{e}", align_bytes=64) for e in range(E)]
@@ -76,7 +76,6 @@ def tile_moe_bdx_glu_relu_kernel(
         nc.gpsimd.affine_select(
             out=ident[:], in_=ident[:], compare_op=ALU.not_equal, fill=1.0, base=0, pattern=[[-1, P]], channel_multiplier=1
         )
-        w2_s.append(w2_s_last)
 
         def stage_scale_rows(plane, rows):
             nc.sync.dma_start(out=plane[0:P:8].bitcast(I32), in_=rows.rearrange("a f i -> f a i").bitcast(I32))
@@ -104,15 +103,14 @@ def tile_moe_bdx_glu_relu_kernel(
             nc.sync.dma_start(out=dy_w[o][:], in_=dy_words[o].rearrange("p t d -> p (t d)").bitcast(I32))
         load_scale_rows(dy_s, dy_scales)
         load_words(w2_w[0], w2_words, *W2_PARTS[0])
-        stage_scale_rows(w2_s_last, w2_rows(*PAIRS[2]))
+        load_scale_rows(w2_s[0], w2_rows(*W2_SCALE_PARTS[0]))
+        load_words(w2_w[1], w2_words, *W2_PARTS[1])
+        load_saved(a1_t[0], a1, *PAIRS[0])
         stage_scale_rows(w1_s, w1_scales.rearrange("e s f k -> (e s) f k"))
         stage_scale_rows(w3_s, w3_scales.rearrange("e s f k -> (e s) f k"))
         place_scale_rows(late_s)
-        load_scale_rows(w2_s[0], w2_rows(*PAIRS[0]))
-        load_words(w2_w[1], w2_words, *W2_PARTS[1])
-        load_saved(a1_t[0], a1, *PAIRS[0])
         load_words(w2_w[2], w2_words, *W2_PARTS[2])
-        load_scale_rows(w2_s[1], w2_rows(*PAIRS[1]))
+        load_scale_rows(w2_s[1], w2_rows(*W2_SCALE_PARTS[1]))
         load_saved(a3_t[0], a3, *A3_PARTS[0])
         load_saved(a1_t[1], a1, *PAIRS[1])
         load_words(w2_w[3], w2_words, *W2_PARTS[3])
@@ -151,6 +149,7 @@ def tile_moe_bdx_glu_relu_kernel(
         def first_product(e):
             slots = slice(e * C, (e + 1) * C)
             g, j = place(W2_PARTS, e)
+            gs, js = place(W2_SCALE_PARTS, e)
             dh_ps = ps_sum.tile([P, H], F32, name="dh_ps", tag="sum")
             for o in range(PASSES):
                 nc.tensor.matmul_mx(
@@ -158,7 +157,7 @@ def tile_moe_bdx_glu_relu_kernel(
                     lhsT=g_w[o][:, slots].bitcast(FP8X4),
                     lhsT_scale=g_s[o][:, slots],
                     rhs=w2_w[g][:, j * PASSES + o, :].bitcast(FP4X4),
-                    rhs_scale=w2_s[e // 2][:, e % 2 * PASSES + o, :],
+                    rhs_scale=w2_s[gs][:, js * PASSES + o, :],
                     start=(o == 0),
                     stop=(o == PASSES - 1),
                 )

@@ -22,8 +22,8 @@ P = 128
 PACK = 4
 PASSES = N // (P * PACK)
 PAIRS = [(0, 2), (2, 4), (4, 6)]
-W2_SCALE_PARTS = [(0, 2), (2, 6)]
-W2_PARTS = [(0, 1), (1, 2), (2, 4), (4, 6)]
+W2_SCALE_PARTS = PAIRS
+W2_PARTS = [(0, 1), (1, 2), (2, 4), (4, 5), (5, 6)]
 A3_PARTS = [(0, 2), (2, 4), (4, 5), (5, 6)]
 FIRST_SLOTS = 2 * C
 
@@ -48,9 +48,6 @@ def tile_moe_bdx_glu_relu_kernel(
         w2_s = [keep.tile([P, (hi - lo) * PASSES, H], U8, name=f"w2_s{lo}", align_bytes=64) for lo, hi in W2_SCALE_PARTS]
         w1_w = [keep.tile([P, hi - lo, 2 * K], U8, name=f"w1_w{lo}", align_bytes=64) for lo, hi in PAIRS]
         w3_w = [keep.tile([P, hi - lo, 2 * K], U8, name=f"w3_w{lo}", align_bytes=64) for lo, hi in PAIRS]
-        late_s = keep.tile([P, 2 * E * K], U8, name="late_s", align_bytes=64)
-        w1_s = late_s[:, 0 : E * K].rearrange("p (e k) -> p e k", k=K)
-        w3_s = late_s[:, E * K :].rearrange("p (e k) -> p e k", k=K)
         a1_t = [keep.tile([P, PACK, (hi - lo) * C], F32, name=f"a1_t{lo}") for lo, hi in PAIRS]
         a3_t = [keep.tile([P, PACK, (hi - lo) * C], F32, name=f"a3_t{lo}", tag=f"a3_t{lo}") for lo, hi in A3_PARTS]
         codes = [keep.tile([P, 2, C], U32, name=f"codes{e}", align_bytes=64) for e in range(E)]
@@ -72,13 +69,17 @@ def tile_moe_bdx_glu_relu_kernel(
         nc.gpsimd.memset(gate_rows[:], 0.0)
         nc.scalar.dma_start(out=gate_rows[0:E, :], in_=gate[0].rearrange("(e c) -> e c", c=C))
         nc.scalar.activation(result[:], zeros[:, 0:1].to_broadcast([P, T]), ACT.Copy)
-        nc.gpsimd.memset(ident[:], 0.0)
+        blank = keep.tile([P, P], F32, name="blank", tag="reused", align_bytes=64)
+        nc.gpsimd.memset(blank[:], 0.0)
         nc.gpsimd.affine_select(
-            out=ident[:], in_=ident[:], compare_op=ALU.not_equal, fill=1.0, base=0, pattern=[[-1, P]], channel_multiplier=1
+            out=ident[:], in_=blank[:], compare_op=ALU.not_equal, fill=1.0, base=0, pattern=[[-1, P]], channel_multiplier=1
         )
+        late_s = keep.tile([P, 2 * E * K], U8, name="late_s", tag="reused", align_bytes=64)
+        w1_s = late_s[:, 0 : E * K].rearrange("p (e k) -> p e k", k=K)
+        w3_s = late_s[:, E * K :].rearrange("p (e k) -> p e k", k=K)
 
-        def stage_scale_rows(plane, rows):
-            nc.sync.dma_start(out=plane[0:P:8].bitcast(I32), in_=rows.rearrange("a f i -> f a i").bitcast(I32))
+        def stage_scale_rows(plane, rows, queue):
+            queue.dma_start(out=plane[0:P:8].bitcast(I32), in_=rows.rearrange("a f i -> f a i").bitcast(I32))
 
         def place_scale_rows(tile):
             for r in range(1, 4):
@@ -98,6 +99,7 @@ def tile_moe_bdx_glu_relu_kernel(
         def w2_rows(lo, hi):
             return w2_scales[lo:hi].rearrange("e s f i -> (e s) f i")
 
+        stage_scale_rows(w3_s, w3_scales.rearrange("e s f k -> (e s) f k"), nc.gpsimd)
         nc.sync.dma_start(offsets[:], offs)
         for o in range(PASSES):
             nc.sync.dma_start(out=dy_w[o][:], in_=dy_words[o].rearrange("p t d -> p (t d)").bitcast(I32))
@@ -106,14 +108,15 @@ def tile_moe_bdx_glu_relu_kernel(
         load_scale_rows(w2_s[0], w2_rows(*W2_SCALE_PARTS[0]))
         load_words(w2_w[1], w2_words, *W2_PARTS[1])
         load_saved(a1_t[0], a1, *PAIRS[0])
-        stage_scale_rows(w1_s, w1_scales.rearrange("e s f k -> (e s) f k"))
-        stage_scale_rows(w3_s, w3_scales.rearrange("e s f k -> (e s) f k"))
+        stage_scale_rows(w1_s, w1_scales.rearrange("e s f k -> (e s) f k"), nc.sync)
         place_scale_rows(late_s)
         load_words(w2_w[2], w2_words, *W2_PARTS[2])
         load_scale_rows(w2_s[1], w2_rows(*W2_SCALE_PARTS[1]))
         load_saved(a3_t[0], a3, *A3_PARTS[0])
         load_saved(a1_t[1], a1, *PAIRS[1])
         load_words(w2_w[3], w2_words, *W2_PARTS[3])
+        load_scale_rows(w2_s[2], w2_rows(*W2_SCALE_PARTS[2]))
+        load_words(w2_w[4], w2_words, *W2_PARTS[4])
         load_saved(a3_t[1], a3, *A3_PARTS[1])
         load_words(w1_w[0], w1_words, *PAIRS[0])
         load_words(w3_w[0], w3_words, *PAIRS[0])

@@ -26,6 +26,7 @@ W2_SCALE_PARTS = PAIRS
 W2_PARTS = [(0, 1), (1, 2), (2, 4), (4, 5), (5, 6)]
 A3_PARTS = [(0, 2), (2, 4), (4, 5), (5, 6)]
 FIRST_SLOTS = 2 * C
+HALF = H // 2
 
 
 def tile_moe_bdx_glu_relu_kernel(
@@ -35,8 +36,8 @@ def tile_moe_bdx_glu_relu_kernel(
     with ExitStack() as ctx:
         keep = ctx.enter_context(tc.tile_pool(name="keep", bufs=1))
         ring = ctx.enter_context(tc.tile_pool(name="ring", bufs=3))
-        ps_sum = ctx.enter_context(tc.psum_pool(name="ps_sum", bufs=2))
-        ps_turn = ctx.enter_context(tc.psum_pool(name="ps_turn", bufs=E))
+        ps_sum = ctx.enter_context(tc.psum_pool(name="ps_sum", bufs=4))
+        ps_turn = ctx.enter_context(tc.psum_pool(name="ps_turn", bufs=4))
 
         def place(parts, e):
             return [(g, e - lo) for g, (lo, hi) in enumerate(parts) if lo <= e < hi][0]
@@ -153,21 +154,25 @@ def tile_moe_bdx_glu_relu_kernel(
             slots = slice(e * C, (e + 1) * C)
             g, j = place(W2_PARTS, e)
             gs, js = place(W2_SCALE_PARTS, e)
-            dh_ps = ps_sum.tile([P, H], F32, name="dh_ps", tag="sum")
-            for o in range(PASSES):
-                nc.tensor.matmul_mx(
-                    out=dh_ps[:],
-                    lhsT=g_w[o][:, slots].bitcast(FP8X4),
-                    lhsT_scale=g_s[o][:, slots],
-                    rhs=w2_w[g][:, j * PASSES + o, :].bitcast(FP4X4),
-                    rhs_scale=w2_s[gs][:, js * PASSES + o, :],
-                    start=(o == 0),
-                    stop=(o == PASSES - 1),
-                )
             dh_rows = ring.tile([P, PACK, P], F32, name="dh_rows")
-            nc.scalar.activation(
-                dh_rows[:], dh_ps[:].rearrange("s (m t) -> s t m", t=PACK), ACT.Copy, scale=gate_cols[:, e : e + 1]
-            )
+            for h in range(2):
+                dh_ps = ps_sum.tile([P, HALF], F32, name="dh_ps", tag="sum")
+                for o in range(PASSES):
+                    nc.tensor.matmul_mx(
+                        out=dh_ps[:],
+                        lhsT=g_w[o][:, slots].bitcast(FP8X4),
+                        lhsT_scale=g_s[o][:, slots],
+                        rhs=w2_w[g][:, j * PASSES + o, 2 * h * HALF : 2 * (h + 1) * HALF].bitcast(FP4X4),
+                        rhs_scale=w2_s[gs][:, js * PASSES + o, h * HALF : (h + 1) * HALF],
+                        start=(o == 0),
+                        stop=(o == PASSES - 1),
+                    )
+                nc.scalar.activation(
+                    dh_rows[:, :, h * HALF // PACK : (h + 1) * HALF // PACK],
+                    dh_ps[:].rearrange("s (m t) -> s t m", t=PACK),
+                    ACT.Copy,
+                    scale=gate_cols[:, e : e + 1],
+                )
             turned[e] = ps_turn.tile([P, PACK, C], F32, name="turned")
             for t in range(PACK):
                 nc.tensor.transpose(turned[e][:, t, :], dh_rows[:, t, :], ident[:])
@@ -194,20 +199,21 @@ def tile_moe_bdx_glu_relu_kernel(
                 in_=da[e][:].rearrange("p j s t -> p (j s t)"),
             )
 
-        def second_product(e, columns):
-            g, i = place(PAIRS, e)
-            dx_ps = ps_sum.tile([P, C], F32, name="dx_ps", tag="sum")
-            for j, (words, plane) in enumerate(((w1_w, w1_s), (w3_w, w3_s))):
-                nc.tensor.matmul_mx(
-                    out=dx_ps[:],
-                    lhsT=words[g][:, i, :].bitcast(FP4X4),
-                    lhsT_scale=plane[:, e, :],
-                    rhs=codes[e][:, j, :].bitcast(FP8X4),
-                    rhs_scale=scales[e][:, j, :],
-                    start=(j == 0),
-                    stop=(j == 1),
-                )
-            nc.scalar.copy(columns, dx_ps[:])
+        def second_product(lo, hi, columns):
+            dx_ps = ps_sum.tile([P, hi - lo, C], F32, name="dx_ps", tag="sum")
+            for e in range(lo, hi):
+                g, i = place(PAIRS, e)
+                for j, (words, plane) in enumerate(((w1_w, w1_s), (w3_w, w3_s))):
+                    nc.tensor.matmul_mx(
+                        out=dx_ps[:, e - lo, :],
+                        lhsT=words[g][:, i, :].bitcast(FP4X4),
+                        lhsT_scale=plane[:, e, :],
+                        rhs=codes[e][:, j, :].bitcast(FP8X4),
+                        rhs_scale=scales[e][:, j, :],
+                        start=(j == 0),
+                        stop=(j == 1),
+                    )
+            nc.scalar.copy(columns, dx_ps[:].rearrange("p e c -> p (e c)"))
 
         def da3(e):
             gradient(e, 1, saved_columns(a1_t, PAIRS, e))
@@ -231,11 +237,10 @@ def tile_moe_bdx_glu_relu_kernel(
         da1(E - 1)
         quantise(E - 1)
         for lo, hi in PAIRS[:-1]:
-            for e in range(lo, hi):
-                second_product(e, dx[:, e * C : (e + 1) * C])
+            second_product(lo, hi, dx[:, lo * C : hi * C])
             nc.scalar.activation(result[:].indirect(listed(lo * C, hi * C)), dx[:, lo * C : hi * C], ACT.Copy)
         for e, tag in ((E - 2, f"a3_t{E - 1}"), (E - 1, "dx_last")):
             dx_one = keep.tile([P, C], F32, name=f"dx{e}", tag=tag)
-            second_product(e, dx_one[:])
+            second_product(e, e + 1, dx_one[:])
             nc.vector.tensor_tensor(result[:].indirect(listed(e * C, (e + 1) * C)), dx_one[:], zeros[:], ALU.add)
         nc.sync.dma_start(out=out, in_=result[:])

@@ -46,7 +46,7 @@ def tile_moe_bdx_glu_relu_kernel(
         dy_w = [keep.tile([P, T], I32, name=f"dy_w{o}", align_bytes=64) for o in range(PASSES)]
         dy_s = keep.tile([P, PASSES, T], U8, name="dy_s", align_bytes=64)
         w2_w = [keep.tile([P, (hi - lo) * PASSES, 2 * H], U8, name=f"w2_w{lo}", align_bytes=64) for lo, hi in W2_PARTS]
-        w2_s = [keep.tile([P, (hi - lo) * PASSES, H], U8, name=f"w2_s{lo}", align_bytes=64) for lo, hi in W2_SCALE_PARTS]
+        w2_s = [keep.tile([P, (hi - lo) * PASSES, H], U8, name=f"w2_s{lo}", align_bytes=64) for lo, hi in W2_SCALE_PARTS[:-1]]
         w1_w = [keep.tile([P, hi - lo, 2 * K], U8, name=f"w1_w{lo}", align_bytes=64) for lo, hi in PAIRS]
         w3_w = [keep.tile([P, hi - lo, 2 * K], U8, name=f"w3_w{lo}", align_bytes=64) for lo, hi in PAIRS]
         a1_t = [keep.tile([P, PACK, (hi - lo) * C], F32, name=f"a1_t{lo}") for lo, hi in PAIRS]
@@ -75,9 +75,11 @@ def tile_moe_bdx_glu_relu_kernel(
         nc.gpsimd.affine_select(
             out=ident[:], in_=blank[:], compare_op=ALU.not_equal, fill=1.0, base=0, pattern=[[-1, P]], channel_multiplier=1
         )
-        late_s = keep.tile([P, 2 * E * K], U8, name="late_s", tag="reused", align_bytes=64)
+        planes = keep.tile([P, 2 * E * K + 2 * PASSES * H], U8, name="planes", tag="reused", align_bytes=64)
+        late_s = planes[:, 0 : 2 * E * K]
         w1_s = late_s[:, 0 : E * K].rearrange("p (e k) -> p e k", k=K)
         w3_s = late_s[:, E * K :].rearrange("p (e k) -> p e k", k=K)
+        w2_s.append(planes[:, 2 * E * K :].rearrange("p (a i) -> p a i", i=H))
 
         def stage_scale_rows(plane, rows, queue):
             queue.dma_start(out=plane[0:P:8].bitcast(I32), in_=rows.rearrange("a f i -> f a i").bitcast(I32))
@@ -86,10 +88,10 @@ def tile_moe_bdx_glu_relu_kernel(
             for r in range(1, 4):
                 nc.gpsimd.dma_start(out=tile[r:P:32, :].bitcast(I32), in_=tile[8 * r : P : 32, :].bitcast(I32))
 
-        def load_scale_rows(plane, rows):
+        def load_scale_rows(plane, rows, queue=nc.sync, which=range(4)):
             by_r = rows.rearrange("a (q r) i -> r q a i", r=4)
-            for r in range(4):
-                nc.sync.dma_start(out=plane[r:P:32].bitcast(I32), in_=by_r[r].bitcast(I32))
+            for r in which:
+                queue.dma_start(out=plane[r:P:32].bitcast(I32), in_=by_r[r].bitcast(I32))
 
         def load_words(tile, words, lo, hi):
             nc.sync.dma_start(out=tile[:].bitcast(I32), in_=words[lo:hi].rearrange("e s p b -> p (e s) b").bitcast(I32))
@@ -101,6 +103,7 @@ def tile_moe_bdx_glu_relu_kernel(
             return w2_scales[lo:hi].rearrange("e s f i -> (e s) f i")
 
         stage_scale_rows(w3_s, w3_scales.rearrange("e s f k -> (e s) f k"), nc.gpsimd)
+        load_scale_rows(w2_s[2], w2_rows(*W2_SCALE_PARTS[2]), nc.gpsimd, range(2))
         nc.sync.dma_start(offsets[:], offs)
         for o in range(PASSES):
             nc.sync.dma_start(out=dy_w[o][:], in_=dy_words[o].rearrange("p t d -> p (t d)").bitcast(I32))
@@ -116,7 +119,7 @@ def tile_moe_bdx_glu_relu_kernel(
         load_saved(a3_t[0], a3, *A3_PARTS[0])
         load_saved(a1_t[1], a1, *PAIRS[1])
         load_words(w2_w[3], w2_words, *W2_PARTS[3])
-        load_scale_rows(w2_s[2], w2_rows(*W2_SCALE_PARTS[2]))
+        load_scale_rows(w2_s[2], w2_rows(*W2_SCALE_PARTS[2]), nc.sync, range(2, 4))
         load_words(w2_w[4], w2_words, *W2_PARTS[4])
         load_saved(a3_t[1], a3, *A3_PARTS[1])
         load_words(w1_w[0], w1_words, *PAIRS[0])

@@ -188,11 +188,11 @@ def tile_moe_bdx_glu_relu_kernel(
             da[e] = ring.tile([P, 2, C, PACK], BF16, name="da", align_bytes=64)
 
         def by_pairs(planes):
-            return planes.rearrange("p t (c i) -> p c t i", i=2)
+            return planes.rearrange("p t (c i) -> p c t i", i=4)
 
         def gradient(e, j, factor):
             nc.vector.tensor_tensor(
-                da[e][:, j].rearrange("p (c i) t -> p c t i", i=2), by_pairs(masked[e][:]), by_pairs(factor), ALU.mult
+                da[e][:, j].rearrange("p (c i) t -> p c t i", i=4), by_pairs(masked[e][:]), by_pairs(factor), ALU.mult
             )
 
         def quantise(e):

from contextlib import ExitStack

import concourse.mybir as mybir

K, T, E, C, H, N = 128, 1536, 6, 128, 512, 1024
SLOTS = E * C
FLOPS = 2 * SLOTS * (N * H + 2 * H * K)
BYTES = 2 * 128 * T * 4 + 2 * 16 * T + 2 * H * SLOTS * 4 + E * (N * H + 2 * H * K) * 17 // 32 + SLOTS * 4 + 128 * SLOTS // 8 + K * T * 4

F32 = mybir.dt.float32
BF16 = mybir.dt.bfloat16
I32 = mybir.dt.int32
U32 = mybir.dt.uint32
U16 = mybir.dt.uint16
U8 = mybir.dt.uint8
FP8X4 = mybir.dt.float8_e4m3fn_x4
FP4X4 = mybir.dt.float4_e2m1fn_x4
ALU = mybir.AluOpType
ACT = mybir.ActivationFunctionType

P = 128
PACK = 4
PASSES = N // (P * PACK)
PAIRS = [(0, 2), (2, 4), (4, 6)]
W2_SCALE_PARTS = PAIRS
W2_PARTS = [(0, 1), (1, 2), (2, 4), (4, 5), (5, 6)]
A3_PARTS = [(0, 2), (2, 4), (4, 5), (5, 6)]
FIRST_SLOTS = 2 * C
HALF = H // 2


def tile_moe_bdx_glu_relu_kernel(
    tc, dy_words, dy_scales, a1, a3, w2_words, w2_scales, w1_words, w1_scales, w3_words, w3_scales, gate, offs, out
):
    nc = tc.nc
    with ExitStack() as ctx:
        keep = ctx.enter_context(tc.tile_pool(name="keep", bufs=1))
        ring = ctx.enter_context(tc.tile_pool(name="ring", bufs=3))
        ps_sum = ctx.enter_context(tc.psum_pool(name="ps_sum", bufs=4))
        ps_turn = ctx.enter_context(tc.psum_pool(name="ps_turn", bufs=4))

        def place(parts, e):
            return [(g, e - lo) for g, (lo, hi) in enumerate(parts) if lo <= e < hi][0]

        offsets = keep.tile([P, SLOTS // 16], U16, name="offsets")
        dy_w = [keep.tile([P, T], I32, name=f"dy_w{o}", align_bytes=64) for o in range(PASSES)]
        dy_s = keep.tile([P, PASSES, T], U8, name="dy_s", align_bytes=64)
        w2_w = [keep.tile([P, (hi - lo) * PASSES, 2 * H], U8, name=f"w2_w{lo}", align_bytes=64) for lo, hi in W2_PARTS]
        w2_s = [keep.tile([P, (hi - lo) * PASSES, H], U8, name=f"w2_s{lo}", align_bytes=64) for lo, hi in W2_SCALE_PARTS[:-1]]
        w1_w = [keep.tile([P, hi - lo, 2 * K], U8, name=f"w1_w{lo}", align_bytes=64) for lo, hi in PAIRS]
        w3_w = [keep.tile([P, hi - lo, 2 * K], U8, name=f"w3_w{lo}", align_bytes=64) for lo, hi in PAIRS]
        a1_t = [keep.tile([P, PACK, (hi - lo) * C], F32, name=f"a1_t{lo}") for lo, hi in PAIRS]
        a3_t = [keep.tile([P, PACK, (hi - lo) * C], F32, name=f"a3_t{lo}", tag=f"a3_t{lo}") for lo, hi in A3_PARTS]
        codes = [keep.tile([P, 2, C], U32, name=f"codes{e}", align_bytes=64) for e in range(E)]
        scales = [keep.tile([P, 2, C], U8, name=f"scales{e}", align_bytes=64) for e in range(E)]
        gate_rows = keep.tile([P, C], F32, name="gate_rows")
        gate_cols = keep.tile([P, E], F32, name="gate_cols")
        ident = keep.tile([P, P], F32, name="ident")
        zeros = keep.tile([P, C], F32, name="zeros")
        g_w = [keep.tile([P, SLOTS], U32, name=f"g_w{o}", align_bytes=64) for o in range(PASSES)]
        g_s = [keep.tile([P, SLOTS], U8, name=f"g_s{o}", align_bytes=64) for o in range(PASSES)]
        dx = keep.tile([P, SLOTS - 2 * C], F32, name="dx")
        result = keep.tile([P, T], F32, name="result")

        def zero(plane):
            nc.vector.memset(plane[:].rearrange("p a i -> p (a i)").bitcast(I32), 0)

        zero(dy_s)
        nc.vector.memset(zeros[:], 0.0)
        nc.gpsimd.memset(gate_rows[:], 0.0)
        nc.scalar.dma_start(out=gate_rows[0:E, :], in_=gate[0].rearrange("(e c) -> e c", c=C))
        nc.scalar.activation(result[:], zeros[:, 0:1].to_broadcast([P, T]), ACT.Copy)
        blank = keep.tile([P, P], F32, name="blank", tag="reused", align_bytes=64)
        nc.gpsimd.memset(blank[:], 0.0)
        nc.gpsimd.affine_select(
            out=ident[:], in_=blank[:], compare_op=ALU.not_equal, fill=1.0, base=0, pattern=[[-1, P]], channel_multiplier=1
        )
        planes = keep.tile([P, 2 * E * K + 2 * PASSES * H], U8, name="planes", tag="reused", align_bytes=64)
        late_s = planes[:, 0 : 2 * E * K]
        w1_s = late_s[:, 0 : E * K].rearrange("p (e k) -> p e k", k=K)
        w3_s = late_s[:, E * K :].rearrange("p (e k) -> p e k", k=K)
        w2_s.append(planes[:, 2 * E * K :].rearrange("p (a i) -> p a i", i=H))

        def stage_scale_rows(plane, rows, queue):
            queue.dma_start(out=plane[0:P:8].bitcast(I32), in_=rows.rearrange("a f i -> f a i").bitcast(I32))

        def place_scale_rows(tile):
            for r in range(1, 4):
                nc.gpsimd.dma_start(out=tile[r:P:32, :].bitcast(I32), in_=tile[8 * r : P : 32, :].bitcast(I32))

        def load_scale_rows(plane, rows, queue=nc.sync, which=range(4)):
            by_r = rows.rearrange("a (q r) i -> r q a i", r=4)
            for r in which:
                queue.dma_start(out=plane[r:P:32].bitcast(I32), in_=by_r[r].bitcast(I32))

        def load_words(tile, words, lo, hi):
            nc.sync.dma_start(out=tile[:].bitcast(I32), in_=words[lo:hi].rearrange("e s p b -> p (e s) b").bitcast(I32))

        def load_saved(tile, saved, lo, hi):
            nc.sync.dma_start(out=tile[:], in_=saved.rearrange("(p t) s -> p t s", t=PACK)[:, :, lo * C : hi * C])

        def w2_rows(lo, hi):
            return w2_scales[lo:hi].rearrange("e s f i -> (e s) f i")

        stage_scale_rows(w3_s, w3_scales.rearrange("e s f k -> (e s) f k"), nc.gpsimd)
        load_scale_rows(w2_s[2], w2_rows(*W2_SCALE_PARTS[2]), nc.gpsimd, range(2))
        nc.sync.dma_start(offsets[:], offs)
        for o in range(PASSES):
            nc.sync.dma_start(out=dy_w[o][:], in_=dy_words[o].rearrange("p t d -> p (t d)").bitcast(I32))
        load_scale_rows(dy_s, dy_scales)
        load_words(w2_w[0], w2_words, *W2_PARTS[0])
        load_scale_rows(w2_s[0], w2_rows(*W2_SCALE_PARTS[0]))
        load_words(w2_w[1], w2_words, *W2_PARTS[1])
        load_saved(a1_t[0], a1, *PAIRS[0])
        stage_scale_rows(w1_s, w1_scales.rearrange("e s f k -> (e s) f k"), nc.sync)
        place_scale_rows(late_s)
        load_words(w2_w[2], w2_words, *W2_PARTS[2])
        load_scale_rows(w2_s[1], w2_rows(*W2_SCALE_PARTS[1]))
        load_saved(a3_t[0], a3, *A3_PARTS[0])
        load_saved(a1_t[1], a1, *PAIRS[1])
        load_words(w2_w[3], w2_words, *W2_PARTS[3])
        load_scale_rows(w2_s[2], w2_rows(*W2_SCALE_PARTS[2]), nc.sync, range(2, 4))
        load_words(w2_w[4], w2_words, *W2_PARTS[4])
        load_saved(a3_t[1], a3, *A3_PARTS[1])
        load_words(w1_w[0], w1_words, *PAIRS[0])
        load_words(w3_w[0], w3_words, *PAIRS[0])
        load_saved(a1_t[2], a1, *PAIRS[2])
        load_saved(a3_t[2], a3, *A3_PARTS[2])
        load_words(w1_w[1], w1_words, *PAIRS[1])
        load_words(w3_w[1], w3_words, *PAIRS[1])
        load_words(w1_w[2], w1_words, *PAIRS[2])
        load_words(w3_w[2], w3_words, *PAIRS[2])
        load_saved(a3_t[3], a3, *A3_PARTS[3])

        gate_ps = ps_sum.tile([P, P], F32, name="gate_ps", tag="sum")
        nc.tensor.transpose(gate_ps[:], gate_rows[:], ident[:])
        nc.scalar.activation(gate_cols[:], gate_ps[:, 0:E], ACT.Copy)

        def listed(lo, hi):
            return offsets[:, lo // 16 : hi // 16]

        for o in range(PASSES):
            nc.vector.tensor_copy(g_w[o][:], dy_w[o][:].bitcast(U32).indirect(offsets[:]))
        for lo, hi in ((0, FIRST_SLOTS), (FIRST_SLOTS, SLOTS)):
            for o in range(PASSES):
                nc.vector.tensor_copy(g_s[o][:, lo:hi], dy_s[:, o, :].indirect(listed(lo, hi)))

        turned = {}
        masked = {}
        da = {}

        def saved_columns(tiles, parts, e):
            g, j = place(parts, e)
            return tiles[g][:, :, j * C : (j + 1) * C]

        def first_product(e):
            slots = slice(e * C, (e + 1) * C)
            g, j = place(W2_PARTS, e)
            gs, js = place(W2_SCALE_PARTS, e)
            dh_rows = ring.tile([P, PACK, P], F32, name="dh_rows")
            for h in range(2):
                dh_ps = ps_sum.tile([P, HALF], F32, name="dh_ps", tag="sum")
                for o in range(PASSES):
                    nc.tensor.matmul_mx(
                        out=dh_ps[:],
                        lhsT=g_w[o][:, slots].bitcast(FP8X4),
                        lhsT_scale=g_s[o][:, slots],
                        rhs=w2_w[g][:, j * PASSES + o, 2 * h * HALF : 2 * (h + 1) * HALF].bitcast(FP4X4),
                        rhs_scale=w2_s[gs][:, js * PASSES + o, h * HALF : (h + 1) * HALF],
                        start=(o == 0),
                        stop=(o == PASSES - 1),
                    )
                nc.scalar.activation(
                    dh_rows[:, :, h * HALF // PACK : (h + 1) * HALF // PACK],
                    dh_ps[:].rearrange("s (m t) -> s t m", t=PACK),
                    ACT.Copy,
                    scale=gate_cols[:, e : e + 1],
                )
            turned[e] = ps_turn.tile([P, PACK, C], F32, name="turned")
            for t in range(PACK):
                nc.tensor.transpose(turned[e][:, t, :], dh_rows[:, t, :], ident[:])

        def mask_dh(e):
            masked[e] = ring.tile([P, PACK, C], F32, name="masked")
            nc.vector.scalar_tensor_tensor(
                masked[e][:], saved_columns(a1_t, PAIRS, e), 0.0, turned[e][:], ALU.is_gt, ALU.mult
            )
            da[e] = ring.tile([P, 2, C, PACK], BF16, name="da", align_bytes=64)

        def by_pairs(planes):
            return planes.rearrange("p t (c i) -> p c t i", i=4)

        def gradient(e, j, factor):
            nc.vector.tensor_tensor(
                da[e][:, j].rearrange("p (c i) t -> p c t i", i=4), by_pairs(masked[e][:]), by_pairs(factor), ALU.mult
            )

        def quantise(e):
            nc.vector.quantize_mx(
                out=codes[e][:].rearrange("p j s -> p (j s)").bitcast(FP8X4),
                scales=scales[e][:].rearrange("p j s -> p (j s)"),
                in_=da[e][:].rearrange("p j s t -> p (j s t)"),
            )

        def second_product(lo, hi, columns):
            dx_ps = ps_sum.tile([P, hi - lo, C], F32, name="dx_ps", tag="sum")
            for e in range(lo, hi):
                g, i = place(PAIRS, e)
                for j, (words, plane) in enumerate(((w1_w, w1_s), (w3_w, w3_s))):
                    nc.tensor.matmul_mx(
                        out=dx_ps[:, e - lo, :],
                        lhsT=words[g][:, i, :].bitcast(FP4X4),
                        lhsT_scale=plane[:, e, :],
                        rhs=codes[e][:, j, :].bitcast(FP8X4),
                        rhs_scale=scales[e][:, j, :],
                        start=(j == 0),
                        stop=(j == 1),
                    )
            nc.scalar.copy(columns, dx_ps[:].rearrange("p e c -> p (e c)"))

        def da3(e):
            gradient(e, 1, saved_columns(a1_t, PAIRS, e))

        def da1(e):
            gradient(e, 0, saved_columns(a3_t, A3_PARTS, e))

        for lo, hi in PAIRS:
            for e in range(lo, hi):
                first_product(e)
            for e in range(lo, hi):
                mask_dh(e)
            if hi < E:
                for step in (da3, da1, quantise):
                    for e in range(lo, hi):
                        step(e)
        da3(E - 2)
        da1(E - 2)
        da3(E - 1)
        quantise(E - 2)
        da1(E - 1)
        quantise(E - 1)
        for lo, hi in PAIRS[:-1]:
            second_product(lo, hi, dx[:, lo * C : hi * C])
            nc.scalar.activation(result[:].indirect(listed(lo * C, hi * C)), dx[:, lo * C : hi * C], ACT.Copy)
        for e, tag in ((E - 2, f"a3_t{E - 1}"), (E - 1, "dx_last")):
            dx_one = keep.tile([P, C], F32, name=f"dx{e}", tag=tag)
            second_product(e, e + 1, dx_one[:])
            nc.vector.tensor_tensor(result[:].indirect(listed(e * C, (e + 1) * C)), dx_one[:], zeros[:], ALU.add)
        nc.sync.dma_start(out=out, in_=result[:])
